import numpy as np
import ml_dtypes


def mxq(x, axis, fmt="e4m3"):
    dtype, down = {"e4m3": (ml_dtypes.float8_e4m3fn, 7), "e5m2": (ml_dtypes.float8_e5m2, 14)}[fmt]
    v = np.moveaxis(np.asarray(x, np.float32).astype(ml_dtypes.bfloat16).astype(np.float64), axis, -1)
    blocks = v.reshape(v.shape[:-1] + (-1, 32))
    amax = np.abs(blocks).max(-1, keepdims=True)
    byte = np.maximum(np.where(amax > 0, np.frexp(amax)[1] - 1 + 127, 0) - down, 1)
    scale = np.exp2(byte - 127.0)
    codes = (blocks / scale).astype(np.float32).astype(dtype).astype(np.float64)
    return np.moveaxis((codes * scale).reshape(v.shape), -1, axis)


WIDE = False


def mx_kscale(k):
    if not WIDE:
        return np.ones(k)
    levels = np.array([10, -10, 5, -5, 0])
    if k % 512:
        return np.exp2(np.random.permutation(np.resize(levels, k // 32))).repeat(32)
    a = np.empty((k // 512, 16))
    for p in range(k // 512):
        a[p, :8] = np.random.permutation(np.resize(levels, 8))
        for g in range(8):
            far = levels[np.abs(levels - a[p, g]) >= 10]
            a[p, g + 8] = far[np.random.randint(len(far))]
    return np.exp2(a.ravel()).repeat(32)


def f64(x):
    return np.asarray(x).astype(np.float64)


def striped(idx):
    return np.tile(idx.reshape(-1, 16).T, (8, 1)).astype(np.uint16)


def unstriped(offs):
    return offs[:16].T.reshape(-1).astype(np.int64)


def pack_weight(w):
    k, n = w.shape
    w = f64(np.asarray(w, np.float32).astype(ml_dtypes.bfloat16)).reshape(k // 32, 32, n)
    amax = np.abs(w).max(1)
    byte = np.clip(np.where(amax > 0, np.frexp(amax)[1] - 1 + 127 - 7, 1), 1, 254)
    scaled = (w * np.exp2(127.0 - byte)[:, None, :]).reshape(k, n).astype(np.float32)
    words = np.ascontiguousarray(scaled.reshape(k // 512, 128, 4, n).transpose(0, 1, 3, 2)).astype(ml_dtypes.float8_e4m3fn).view(np.uint8)
    return words, np.ascontiguousarray(byte.astype(np.uint8).reshape(k // 512, 16, n))


def unpack_weight(words, scales):
    g, p, n, _ = words.shape
    vals = np.ascontiguousarray(words).view(ml_dtypes.float8_e4m3fn).astype(np.float64) * np.repeat(np.exp2(scales.astype(np.float64) - 127.0), 8, axis=1)[..., None]
    return vals.transpose(0, 1, 3, 2).reshape(g * 512, n)


def relu(v):
    return np.maximum(v, 0.0)


K, T, S, V, H, N = 512, 2048, 1024, 512, 512, 128


def setup_inputs():
    n = np.random.standard_normal
    s = mx_kscale(K)[:, None]
    u = mx_kscale(H)
    packed_xT = pack_weight(n((K, T)) * s)
    return {
        "x_words": packed_xT[0],
        "x_scales": packed_xT[1],
        "w1": (n((K, H)) / np.sqrt(K) / s * u).astype(np.float32),
        "w2": (n((H, N)) / np.sqrt(2 * H) / u[:, None]).astype(np.float32),
        "w3": (n((H, N)) / np.sqrt(2 * H) / u[:, None]).astype(np.float32),
        "offs": striped(np.random.permutation(T)[:S]),
        "cen": striped(np.random.permutation(S)[:V]),
        "pos1": striped(np.random.permutation(S)[:V]),
        "pos2": striped(np.random.permutation(S)[:V]),
        "pos3": striped(np.random.permutation(S)[:V]),
        "pos4": striped(np.random.permutation(S)[:V]),
    }


def reference(x_words, x_scales, w1, w2, w3, offs, cen, pos1, pos2, pos3, pos4):
    xq = unpack_weight(x_words, x_scales)[:, unstriped(offs)]
    h = relu(mxq(f64(w1), 0, "e4m3").T @ xq)
    hc = h[:, unstriped(cen)]
    z = np.maximum(np.maximum(np.maximum(h[:, unstriped(pos1)], h[:, unstriped(pos2)]), h[:, unstriped(pos3)]), h[:, unstriped(pos4)])
    return mxq(f64(w2), 0, "e4m3").T @ mxq(hc, 0, "e4m3") + mxq(f64(w3), 0, "e4m3").T @ mxq(z, 0, "e4m3")

@@ -1,0 +1,173 @@
+from contextlib import ExitStack
+
+import concourse.mybir as mybir
+
+K, T, S, V, H, N = 512, 2048, 1024, 512, 512, 128
+FLOPS = 2 * K * H * S + 2 * 2 * H * N * V
+
+F32 = mybir.dt.float32
+BF16 = mybir.dt.bfloat16
+I32 = mybir.dt.int32
+U32 = mybir.dt.uint32
+U16 = mybir.dt.uint16
+U8 = mybir.dt.uint8
+FP8X4 = mybir.dt.float8_e4m3fn_x4
+MAX = mybir.AluOpType.max
+RELU = mybir.ActivationFunctionType.Relu
+
+P = 128
+PACK = 4
+BANK = 512
+W1_CHUNKS = ((0, 256), (256, 512))
+GATHER_PIECES = ((0, 384), (384, 512))
+PIECES = ((0, 256), (256, 384), (384, 512))
+
+
+def tile_picked_sagecat_max_p_kernel(tc, x_words, x_scales, w1, w2, w3, offs, cen, pos1, pos2, pos3, pos4, out):
+    nc = tc.nc
+    with ExitStack() as ctx:
+        keep = ctx.enter_context(tc.tile_pool(name="keep", bufs=1))
+        ring = ctx.enter_context(tc.tile_pool(name="ring", bufs=2))
+        psum_h = ctx.enter_context(tc.psum_pool(name="psum_h", bufs=4))
+        psum_o = ctx.enter_context(tc.psum_pool(name="psum_o", bufs=3))
+
+        def load_list(src, name):
+            tile = keep.tile(list(src.shape), U16, name=name)
+            nc.sync.dma_start(tile[:], src)
+            return tile
+
+        table_scales = keep.tile([P, T], U8, align_bytes=64)
+        nc.vector.memset(table_scales[:].bitcast(I32), 0)
+        offs_sb = load_list(offs, "offs_sb")
+        pos_sb = [load_list(pos1, "pos1_sb")]
+        for q in range(4):
+            nc.sync.dma_start(table_scales[32 * q : 32 * q + 4, :].bitcast(I32), x_scales[0, 4 * q : 4 * q + 4, :].bitcast(I32))
+        table_words = keep.tile([P, T], U32, align_bytes=64)
+        nc.sync.dma_start(table_words[:].bitcast(I32), x_words[0].rearrange("p c r -> p (c r)").bitcast(I32))
+        w1_rows = w1.rearrange("(p j) c -> p j c", j=PACK)
+        w1_raw = []
+        for c0, c1 in W1_CHUNKS:
+            raw = keep.tile([P, PACK, c1 - c0], F32, name="w1_raw%d" % c0)
+            nc.sync.dma_start(raw[:], w1_rows[:, :, c0:c1])
+            w1_raw.append(raw)
+        pos_sb.append(load_list(pos2, "pos2_sb"))
+        pos_sb.append(load_list(pos3, "pos3_sb"))
+        pos_sb.append(load_list(pos4, "pos4_sb"))
+        w23_raw = []
+        for a, w in enumerate((w3, w2)):
+            raw = keep.tile([P, PACK, N], F32, name="w23_raw%d" % a)
+            nc.sync.dma_start(raw[:], w.rearrange("(p j) n -> p j n", j=PACK))
+            w23_raw.append(raw)
+        cen_sb = load_list(cen, "cen_sb")
+
+        x_sc = keep.tile([P, S], U8, align_bytes=64)
+        nc.vector.tensor_copy(x_sc[:], table_scales[:].indirect(offs_sb[:]))
+        x_cd = keep.tile([P, S], U32, align_bytes=64)
+        for half in range(S // BANK):
+            nc.vector.tensor_copy(x_cd[:, half * BANK : (half + 1) * BANK], table_words[:].indirect(offs_sb[:, half * BANK // 16 : (half + 1) * BANK // 16]))
+
+        w1_first = keep.tile([P, P, PACK], BF16, align_bytes=64)
+        w1_rest = keep.tile([P, PACK - 1, P, PACK], BF16, align_bytes=64)
+        for raw, (c0, c1), first_copy in zip(w1_raw, W1_CHUNKS, (nc.scalar.copy, nc.vector.tensor_copy)):
+            dealt = raw[:].rearrange("p j (m t) -> p m j t", t=PACK)
+            first_copy(w1_first[:, c0 // PACK : c1 // PACK, :], dealt[:, :, :, 0])
+            nc.scalar.copy(w1_rest[:, :, c0 // PACK : c1 // PACK, :].rearrange("p t m j -> p m j t"), dealt[:, :, :, 1:])
+        w1_bf = [w1_first[:]] + [w1_rest[:, t] for t in range(PACK - 1)]
+
+        h = []
+        for t in range(PACK):
+            w1_cd = keep.tile([P, P], U32, align_bytes=64, name="w1_cd%d" % t)
+            w1_sc = keep.tile([P, P], U8, align_bytes=64, name="w1_sc%d" % t)
+            nc.vector.quantize_mx(out=w1_cd[:].bitcast(FP8X4), scales=w1_sc[:], in_=w1_bf[t].rearrange("p m j -> p (m j)"))
+            ht = keep.tile([P, S], F32, name="h%d" % t)
+            step = BANK // 2 if t == 0 else BANK
+            for n, s0 in enumerate(range(0, S, step)):
+                nodes = slice(s0, s0 + step)
+                acc = psum_h.tile([P, BANK], F32)
+                nc.tensor.matmul_mx(out=acc[:, :step], lhsT=w1_cd[:].bitcast(FP8X4), lhsT_scale=w1_sc[:],
+                                    rhs=x_cd[:, nodes].bitcast(FP8X4), rhs_scale=x_sc[:, nodes], start=True, stop=True)
+                if t == 0 and n % 2 == 1:
+                    nc.vector.tensor_scalar_max(ht[:, nodes], acc[:, :step], 0.0)
+                else:
+                    nc.scalar.activation(ht[:, nodes], acc[:, :step], RELU)
+            h.append(ht)
+
+        w23_bf = keep.tile([P, 2, N, PACK], BF16, align_bytes=64)
+        for a in range(2):
+            nc.scalar.copy(w23_bf[:, a].rearrange("p (c i) j -> p c j i", i=4), w23_raw[a][:].rearrange("p j (c i) -> p c j i", i=4))
+        w23_cd = keep.tile([P, 2 * N], U32, align_bytes=64)
+        w23_sc = keep.tile([P, 2 * N], U8, align_bytes=64)
+        nc.vector.quantize_mx(out=w23_cd[:].bitcast(FP8X4), scales=w23_sc[:], in_=w23_bf[:].rearrange("p a n j -> p (a n j)"))
+
+        z_planes = keep.tile([P, PACK, V], BF16)
+        nbs, pairs = [], []
+
+        def max_of_pairs(t):
+            pair = ring.tile([P, 2 * V], BF16)
+            nc.vector.tensor_tensor(pair[:], nbs[t][:, : 2 * V], nbs[t][:, 2 * V :], MAX)
+            pairs.append(pair)
+
+        def max_of_four(t):
+            nc.vector.tensor_tensor(z_planes[:, t, :], pairs[t][:, :V], pairs[t][:, V:], MAX)
+
+        behind = (max_of_pairs, max_of_four)
+        last = PACK - 1
+        for t in range(last):
+            nb = ring.tile([P, 4 * V], BF16)
+            nbs.append(nb)
+            for d in range(4):
+                nc.vector.tensor_copy(nb[:, d * V : (d + 1) * V], h[t][:].indirect(pos_sb[d][:]))
+                if t > 0 and d < 2:
+                    behind[d](t - 1)
+        nb = ring.tile([P, 4 * V], BF16)
+        running = ring.tile([P, 2 * V], BF16, tag="pair")
+        for d in range(4):
+            nc.vector.tensor_copy(nb[:, d * V : (d + 1) * V], h[last][:].indirect(pos_sb[d][:]))
+            if d < 2:
+                behind[d](last - 1)
+            if d == 2:
+                nc.vector.tensor_tensor(running[:, :V], nb[:, :V], nb[:, V : 2 * V], MAX)
+        nc.vector.tensor_tensor(running[:, V:], running[:, :V], nb[:, 2 * V : 3 * V], MAX)
+
+        def interleave(dst, planes):
+            nc.scalar.copy(dst.rearrange("p (c i) t -> p c t i", i=4), planes.rearrange("p t (c i) -> p c t i", i=4))
+
+        z_bf = keep.tile([P, V, PACK], BF16, align_bytes=64)
+        z_cd = keep.tile([P, V], U32, align_bytes=64)
+        z_sc = keep.tile([P, V], U8, align_bytes=64)
+        c_bf = keep.tile([P, V, PACK], BF16, align_bytes=64)
+        c_cd = keep.tile([P, V], U32, align_bytes=64)
+        c_sc = keep.tile([P, V], U8, align_bytes=64)
+
+        def gather_centres(v0, v1, home):
+            planes = home.rearrange("p (t v) -> p t v", t=PACK)
+            for t in range(PACK):
+                nc.vector.tensor_copy(planes[:, t, :], h[t][:].indirect(cen_sb[:, v0 // 16 : v1 // 16]))
+                if v0 == 0 and t == 0:
+                    nc.vector.tensor_tensor(z_planes[:, last, :], running[:, V:], nb[:, 3 * V :], MAX)
+            return planes
+
+        def open_group(v0, v1):
+            acc_o = psum_o.tile([P, BANK], F32)
+            nc.tensor.matmul_mx(out=acc_o[:, : v1 - v0], lhsT=w23_cd[:, :N].bitcast(FP8X4), lhsT_scale=w23_sc[:, :N],
+                                rhs=z_cd[:, v0:v1].bitcast(FP8X4), rhs_scale=z_sc[:, v0:v1], start=True, stop=False)
+            return acc_o
+
+        def close_group(v0, v1, acc_o, engine_copy):
+            nc.vector.quantize_mx(out=c_cd[:, v0:v1].bitcast(FP8X4), scales=c_sc[:, v0:v1], in_=c_bf[:, v0:v1, :].rearrange("p v t -> p (v t)"))
+            nc.tensor.matmul_mx(out=acc_o[:, : v1 - v0], lhsT=w23_cd[:, N:].bitcast(FP8X4), lhsT_scale=w23_sc[:, N:],
+                                rhs=c_cd[:, v0:v1].bitcast(FP8X4), rhs_scale=c_sc[:, v0:v1], start=False, stop=True)
+            res = keep.tile([P, v1 - v0], F32, name="res%d" % v0)
+            engine_copy(res[:], acc_o[:, : v1 - v0])
+            nc.sync.dma_start(out[:, v0:v1], res[:])
+
+        (a0, a1), (b0, b1) = GATHER_PIECES
+        planes_a = gather_centres(a0, a1, nbs[last - 1][:, : PACK * a1])
+        interleave(z_bf[:], z_planes[:])
+        nc.vector.quantize_mx(out=z_cd[:].bitcast(FP8X4), scales=z_sc[:], in_=z_bf[:].rearrange("p v t -> p (v t)"))
+        accs = [open_group(v0, v1) for v0, v1 in PIECES]
+        interleave(c_bf[:, a0:a1, :], planes_a)
+        planes_b = gather_centres(b0, b1, z_bf[:, : b1 - b0, :].rearrange("p v t -> p (v t)"))
+        interleave(c_bf[:, b0:b1, :], planes_b)
+        for (v0, v1), acc_o, engine_copy in zip(PIECES, accs, (nc.scalar.copy, nc.scalar.copy, nc.vector.tensor_copy)):
+            close_group(v0, v1, acc_o, engine_copy)

@@ -13,12 +13,14 @@ U16 = mybir.dt.uint16
 U8 = mybir.dt.uint8
 FP8X4 = mybir.dt.float8_e4m3fn_x4
 MAX = mybir.AluOpType.max
+ADD = mybir.AluOpType.add
+SUB = mybir.AluOpType.subtract
 RELU = mybir.ActivationFunctionType.Relu
 
 P = 128
 PACK = 4
 BANK = 512
-W1_CHUNKS = ((0, 256), (256, 512))
+W1_CHUNKS = ((0, 384), (384, 512))
 GATHER_PIECES = ((0, 384), (384, 512))
 PIECES = ((0, 256), (256, 384), (384, 512))
 
@@ -66,30 +68,29 @@ def tile_picked_sagecat_max_p_kernel(tc, x_words, x_scales, w1, w2, w3, offs, ce
         for half in range(S // BANK):
             nc.vector.tensor_copy(x_cd[:, half * BANK : (half + 1) * BANK], table_words[:].indirect(offs_sb[:, half * BANK // 16 : (half + 1) * BANK // 16]))
 
-        w1_first = keep.tile([P, P, PACK], BF16, align_bytes=64)
         w1_rest = keep.tile([P, PACK - 1, P, PACK], BF16, align_bytes=64)
-        for raw, (c0, c1), first_copy in zip(w1_raw, W1_CHUNKS, (nc.scalar.copy, nc.vector.tensor_copy)):
-            dealt = raw[:].rearrange("p j (m t) -> p m j t", t=PACK)
-            first_copy(w1_first[:, c0 // PACK : c1 // PACK, :], dealt[:, :, :, 0])
-            nc.scalar.copy(w1_rest[:, :, c0 // PACK : c1 // PACK, :].rearrange("p t m j -> p m j t"), dealt[:, :, :, 1:])
-        w1_bf = [w1_first[:]] + [w1_rest[:, t] for t in range(PACK - 1)]
+        w1_first = w1_rest[:, 0]
+        dealt = [raw[:].rearrange("p j (m t) -> p m j t", t=PACK) for raw in w1_raw]
+        for src, (c0, c1) in zip(dealt, W1_CHUNKS):
+            nc.scalar.copy(w1_first[:, c0 // PACK : c1 // PACK, :], src[:, :, :, 0])
+        w1_bf = [w1_first] + [w1_rest[:, t] for t in range(PACK - 1)]
 
         h = []
         for t in range(PACK):
             w1_cd = keep.tile([P, P], U32, align_bytes=64, name="w1_cd%d" % t)
             w1_sc = keep.tile([P, P], U8, align_bytes=64, name="w1_sc%d" % t)
             nc.vector.quantize_mx(out=w1_cd[:].bitcast(FP8X4), scales=w1_sc[:], in_=w1_bf[t].rearrange("p m j -> p (m j)"))
+            if t == 0:
+                for src, (c0, c1) in zip(dealt, W1_CHUNKS):
+                    nc.vector.tensor_copy(w1_rest[:, :, c0 // PACK : c1 // PACK, :].rearrange("p t m j -> p m j t"), src[:, :, :, 1:])
             ht = keep.tile([P, S], F32, name="h%d" % t)
             step = BANK // 2 if t == 0 else BANK
-            for n, s0 in enumerate(range(0, S, step)):
+            for s0 in range(0, S, step):
                 nodes = slice(s0, s0 + step)
                 acc = psum_h.tile([P, BANK], F32)
                 nc.tensor.matmul_mx(out=acc[:, :step], lhsT=w1_cd[:].bitcast(FP8X4), lhsT_scale=w1_sc[:],
                                     rhs=x_cd[:, nodes].bitcast(FP8X4), rhs_scale=x_sc[:, nodes], start=True, stop=True)
-                if t == 0 and n % 2 == 1:
-                    nc.vector.tensor_scalar_max(ht[:, nodes], acc[:, :step], 0.0)
-                else:
-                    nc.scalar.activation(ht[:, nodes], acc[:, :step], RELU)
+                nc.scalar.activation(ht[:, nodes], acc[:, :step], RELU)
             h.append(ht)
 
         w23_bf = keep.tile([P, 2, N, PACK], BF16, align_bytes=64)
@@ -100,34 +101,34 @@ def tile_picked_sagecat_max_p_kernel(tc, x_words, x_scales, w1, w2, w3, offs, ce
         nc.vector.quantize_mx(out=w23_cd[:].bitcast(FP8X4), scales=w23_sc[:], in_=w23_bf[:].rearrange("p a n j -> p (a n j)"))
 
         z_planes = keep.tile([P, PACK, V], BF16)
-        nbs, pairs = [], []
-
-        def max_of_pairs(t):
-            pair = ring.tile([P, 2 * V], BF16)
-            nc.vector.tensor_tensor(pair[:], nbs[t][:, : 2 * V], nbs[t][:, 2 * V :], MAX)
-            pairs.append(pair)
-
-        def max_of_four(t):
-            nc.vector.tensor_tensor(z_planes[:, t, :], pairs[t][:, :V], pairs[t][:, V:], MAX)
-
-        behind = (max_of_pairs, max_of_four)
         last = PACK - 1
-        for t in range(last):
-            nb = ring.tile([P, 4 * V], BF16)
-            nbs.append(nb)
-            for d in range(4):
-                nc.vector.tensor_copy(nb[:, d * V : (d + 1) * V], h[t][:].indirect(pos_sb[d][:]))
-                if t > 0 and d < 2:
-                    behind[d](t - 1)
-        nb = ring.tile([P, 4 * V], BF16)
-        running = ring.tile([P, 2 * V], BF16, tag="pair")
+        nb = keep.tile([P, PACK * 6 * V], BF16)
+        pairs = nb[:, PACK * 4 * V :].rearrange("p (e t v) -> p e t v", e=2, t=PACK)
+
+        def slot(t, s, count=1):
+            return nb[:, (4 * t + s) * V : (4 * t + s + count) * V]
+
+        def gather_neighbours(dst, t, d):
+            nc.vector.tensor_copy(dst, h[t][:].indirect(pos_sb[d][:]))
+
+        for t in range(2):
+            for e in range(2):
+                gather_neighbours(slot(t, e), t, 2 * e)
+                gather_neighbours(slot(t, 2 + e), t, 2 * e + 1)
+                diff = ring.tile([P, V], F32, bufs=1)
+                gain = ring.tile([P, V], F32, bufs=1)
+                nc.gpsimd.tensor_tensor(diff[:], slot(t, 2 + e), slot(t, e), SUB)
+                nc.scalar.activation(gain[:], diff[:], RELU)
+                nc.gpsimd.tensor_tensor(pairs[:, e, t, :], slot(t, e), gain[:], ADD)
         for d in range(4):
-            nc.vector.tensor_copy(nb[:, d * V : (d + 1) * V], h[last][:].indirect(pos_sb[d][:]))
-            if d < 2:
-                behind[d](last - 1)
-            if d == 2:
-                nc.vector.tensor_tensor(running[:, :V], nb[:, :V], nb[:, V : 2 * V], MAX)
-        nc.vector.tensor_tensor(running[:, V:], running[:, :V], nb[:, 2 * V : 3 * V], MAX)
+            gather_neighbours(slot(2, d), 2, d)
+        gather_neighbours(slot(last, 0), last, 0)
+        gather_neighbours(slot(last, 3), last, 1)
+        nc.vector.tensor_tensor(pairs[:, :, 2, :], slot(2, 0, 2).rearrange("p (e v) -> p e v", e=2), slot(2, 2, 2).rearrange("p (e v) -> p e v", e=2), MAX)
+        gather_neighbours(slot(last, 2), last, 2)
+        nc.vector.tensor_tensor(slot(last, 1), slot(last, 0), slot(last, 3), MAX)
+        gather_neighbours(pairs[:, 1, last, :], last, 3)
+        nc.vector.tensor_tensor(pairs[:, 0, last, :], slot(last, 1), slot(last, 2), MAX)
 
         def interleave(dst, planes):
             nc.scalar.copy(dst.rearrange("p (c i) t -> p c t i", i=4), planes.rearrange("p t (c i) -> p c t i", i=4))
@@ -135,16 +136,13 @@ def tile_picked_sagecat_max_p_kernel(tc, x_words, x_scales, w1, w2, w3, offs, ce
         z_bf = keep.tile([P, V, PACK], BF16, align_bytes=64)
         z_cd = keep.tile([P, V], U32, align_bytes=64)
         z_sc = keep.tile([P, V], U8, align_bytes=64)
-        c_bf = keep.tile([P, V, PACK], BF16, align_bytes=64)
-        c_cd = keep.tile([P, V], U32, align_bytes=64)
-        c_sc = keep.tile([P, V], U8, align_bytes=64)
 
         def gather_centres(v0, v1, home):
             planes = home.rearrange("p (t v) -> p t v", t=PACK)
             for t in range(PACK):
                 nc.vector.tensor_copy(planes[:, t, :], h[t][:].indirect(cen_sb[:, v0 // 16 : v1 // 16]))
                 if v0 == 0 and t == 0:
-                    nc.vector.tensor_tensor(z_planes[:, last, :], running[:, V:], nb[:, 3 * V :], MAX)
+                    nc.vector.tensor_tensor(z_planes[:], pairs[:, 0], pairs[:, 1], MAX)
             return planes
 
         def open_group(v0, v1):
@@ -153,21 +151,25 @@ def tile_picked_sagecat_max_p_kernel(tc, x_words, x_scales, w1, w2, w3, offs, ce
                                 rhs=z_cd[:, v0:v1].bitcast(FP8X4), rhs_scale=z_sc[:, v0:v1], start=True, stop=False)
             return acc_o
 
-        def close_group(v0, v1, acc_o, engine_copy):
-            nc.vector.quantize_mx(out=c_cd[:, v0:v1].bitcast(FP8X4), scales=c_sc[:, v0:v1], in_=c_bf[:, v0:v1, :].rearrange("p v t -> p (v t)"))
+        def close_group(v0, v1, acc_o, c_bf, engine_copy):
+            c_cd = keep.tile([P, v1 - v0], U32, align_bytes=64, name="c_cd%d" % v0)
+            c_sc = keep.tile([P, v1 - v0], U8, align_bytes=64, name="c_sc%d" % v0)
+            nc.vector.quantize_mx(out=c_cd[:].bitcast(FP8X4), scales=c_sc[:], in_=c_bf[:].rearrange("p v t -> p (v t)"))
             nc.tensor.matmul_mx(out=acc_o[:, : v1 - v0], lhsT=w23_cd[:, N:].bitcast(FP8X4), lhsT_scale=w23_sc[:, N:],
-                                rhs=c_cd[:, v0:v1].bitcast(FP8X4), rhs_scale=c_sc[:, v0:v1], start=False, stop=True)
+                                rhs=c_cd[:].bitcast(FP8X4), rhs_scale=c_sc[:], start=False, stop=True)
             res = keep.tile([P, v1 - v0], F32, name="res%d" % v0)
             engine_copy(res[:], acc_o[:, : v1 - v0])
             nc.sync.dma_start(out[:, v0:v1], res[:])
 
         (a0, a1), (b0, b1) = GATHER_PIECES
-        planes_a = gather_centres(a0, a1, nbs[last - 1][:, : PACK * a1])
+        planes_a = gather_centres(a0, a1, nb[:, 16 * V - a1 : 16 * V + last * a1])
         interleave(z_bf[:], z_planes[:])
         nc.vector.quantize_mx(out=z_cd[:].bitcast(FP8X4), scales=z_sc[:], in_=z_bf[:].rearrange("p v t -> p (v t)"))
         accs = [open_group(v0, v1) for v0, v1 in PIECES]
-        interleave(c_bf[:, a0:a1, :], planes_a)
+        c_bfs = [keep.tile([P, v1 - v0, PACK], BF16, align_bytes=64, name="c_bf%d" % v0) for v0, v1 in PIECES]
+        for (v0, v1), c_bf in zip(PIECES[:-1], c_bfs):
+            interleave(c_bf[:], planes_a[:, :, v0:v1])
         planes_b = gather_centres(b0, b1, z_bf[:, : b1 - b0, :].rearrange("p v t -> p (v t)"))
-        interleave(c_bf[:, b0:b1, :], planes_b)
-        for (v0, v1), acc_o, engine_copy in zip(PIECES, accs, (nc.scalar.copy, nc.scalar.copy, nc.vector.tensor_copy)):
-            close_group(v0, v1, acc_o, engine_copy)
+        interleave(c_bfs[-1][:], planes_b)
+        for (v0, v1), acc_o, c_bf, engine_copy in zip(PIECES, accs, c_bfs, (nc.scalar.copy, nc.scalar.copy, nc.vector.tensor_copy)):
+            close_group(v0, v1, acc_o, c_bf, engine_copy)

@@ -20,7 +20,7 @@ RELU = mybir.ActivationFunctionType.Relu
 P = 128
 PACK = 4
 BANK = 512
-W1_CHUNKS = ((0, 384), (384, 512))
+SCALAR_SHARE = 80
 GATHER_PIECES = ((0, 384), (384, 512))
 PIECES = ((0, 256), (256, 384), (384, 512))
 
@@ -46,12 +46,8 @@ def tile_picked_sagecat_max_p_kernel(tc, x_words, x_scales, w1, w2, w3, offs, ce
             nc.sync.dma_start(table_scales[32 * q : 32 * q + 4, :].bitcast(I32), x_scales[0, 4 * q : 4 * q + 4, :].bitcast(I32))
         table_words = keep.tile([P, T], U32, align_bytes=64)
         nc.sync.dma_start(table_words[:].bitcast(I32), x_words[0].rearrange("p c r -> p (c r)").bitcast(I32))
-        w1_rows = w1.rearrange("(p j) c -> p j c", j=PACK)
-        w1_raw = []
-        for c0, c1 in W1_CHUNKS:
-            raw = keep.tile([P, PACK, c1 - c0], F32, name="w1_raw%d" % c0)
-            nc.sync.dma_start(raw[:], w1_rows[:, :, c0:c1])
-            w1_raw.append(raw)
+        w1_raw = keep.tile([P, PACK, H], F32)
+        nc.sync.dma_start(w1_raw[:], w1.rearrange("(p j) c -> p j c", j=PACK))
         pos_sb.append(load_list(pos2, "pos2_sb"))
         pos_sb.append(load_list(pos3, "pos3_sb"))
         pos_sb.append(load_list(pos4, "pos4_sb"))
@@ -65,14 +61,13 @@ def tile_picked_sagecat_max_p_kernel(tc, x_words, x_scales, w1, w2, w3, offs, ce
         x_sc = keep.tile([P, S], U8, align_bytes=64)
         nc.vector.tensor_copy(x_sc[:], table_scales[:].indirect(offs_sb[:]))
         x_cd = keep.tile([P, S], U32, align_bytes=64)
-        for half in range(S // BANK):
-            nc.vector.tensor_copy(x_cd[:, half * BANK : (half + 1) * BANK], table_words[:].indirect(offs_sb[:, half * BANK // 16 : (half + 1) * BANK // 16]))
+        nc.vector.tensor_copy(x_cd[:], table_words[:].indirect(offs_sb[:]))
 
         w1_rest = keep.tile([P, PACK - 1, P, PACK], BF16, align_bytes=64)
         w1_first = w1_rest[:, 0]
-        dealt = [raw[:].rearrange("p j (m t) -> p m j t", t=PACK) for raw in w1_raw]
-        for src, (c0, c1) in zip(dealt, W1_CHUNKS):
-            nc.scalar.copy(w1_first[:, c0 // PACK : c1 // PACK, :], src[:, :, :, 0])
+        dealt = w1_raw[:].rearrange("p j (m t) -> p m j t", t=PACK)
+        nc.scalar.copy(w1_first[:, :SCALAR_SHARE, :], dealt[:, :SCALAR_SHARE, :, 0])
+        nc.vector.tensor_copy(w1_first[:, SCALAR_SHARE:, :], dealt[:, SCALAR_SHARE:, :, 0])
         w1_bf = [w1_first] + [w1_rest[:, t] for t in range(PACK - 1)]
 
         h = []
@@ -81,8 +76,7 @@ def tile_picked_sagecat_max_p_kernel(tc, x_words, x_scales, w1, w2, w3, offs, ce
             w1_sc = keep.tile([P, P], U8, align_bytes=64, name="w1_sc%d" % t)
             nc.vector.quantize_mx(out=w1_cd[:].bitcast(FP8X4), scales=w1_sc[:], in_=w1_bf[t].rearrange("p m j -> p (m j)"))
             if t == 0:
-                for src, (c0, c1) in zip(dealt, W1_CHUNKS):
-                    nc.vector.tensor_copy(w1_rest[:, :, c0 // PACK : c1 // PACK, :].rearrange("p t m j -> p m j t"), src[:, :, :, 1:])
+                nc.vector.tensor_copy(w1_rest[:].rearrange("p t m j -> p m j t"), dealt[:, :, :, 1:])
             ht = keep.tile([P, S], F32, name="h%d" % t)
             step = BANK // 2 if t == 0 else BANK
             for s0 in range(0, S, step):
@@ -93,42 +87,47 @@ def tile_picked_sagecat_max_p_kernel(tc, x_words, x_scales, w1, w2, w3, offs, ce
                 nc.scalar.activation(ht[:, nodes], acc[:, :step], RELU)
             h.append(ht)
 
-        w23_bf = keep.tile([P, 2, N, PACK], BF16, align_bytes=64)
-        for a in range(2):
-            nc.scalar.copy(w23_bf[:, a].rearrange("p (c i) j -> p c j i", i=4), w23_raw[a][:].rearrange("p j (c i) -> p c j i", i=4))
-        w23_cd = keep.tile([P, 2 * N], U32, align_bytes=64)
-        w23_sc = keep.tile([P, 2 * N], U8, align_bytes=64)
-        nc.vector.quantize_mx(out=w23_cd[:].bitcast(FP8X4), scales=w23_sc[:], in_=w23_bf[:].rearrange("p a n j -> p (a n j)"))
-
-        z_planes = keep.tile([P, PACK, V], BF16)
         last = PACK - 1
-        nb = keep.tile([P, PACK * 6 * V], BF16)
+        z_planes = keep.tile([P, PACK, V], BF16)
+        nb = keep.tile([P, PACK * 6 * V], BF16, align_bytes=64)
         pairs = nb[:, PACK * 4 * V :].rearrange("p (e t v) -> p e t v", e=2, t=PACK)
 
-        def slot(t, s, count=1):
-            return nb[:, (4 * t + s) * V : (4 * t + s + count) * V]
+        def slot(s, count=1):
+            return nb[:, s * V : (s + count) * V]
 
         def gather_neighbours(dst, t, d):
             nc.vector.tensor_copy(dst, h[t][:].indirect(pos_sb[d][:]))
 
-        for t in range(2):
-            for e in range(2):
-                gather_neighbours(slot(t, e), t, 2 * e)
-                gather_neighbours(slot(t, 2 + e), t, 2 * e + 1)
-                diff = ring.tile([P, V], F32, bufs=1)
-                gain = ring.tile([P, V], F32, bufs=1)
-                nc.gpsimd.tensor_tensor(diff[:], slot(t, 2 + e), slot(t, e), SUB)
-                nc.scalar.activation(gain[:], diff[:], RELU)
-                nc.gpsimd.tensor_tensor(pairs[:, e, t, :], slot(t, e), gain[:], ADD)
+        units = [(t, e) for t in range(last) for e in range(2)]
+        gains = []
+
+        def add_gain(u):
+            t, e = units[u]
+            nc.gpsimd.tensor_tensor(pairs[:, e, t, :], slot(4 + 2 * u + 1), gains[u][:], ADD)
+
+        for u, (t, e) in enumerate(units):
+            gather_neighbours(slot(4 + 2 * u + 1), t, 2 * e)
+            gather_neighbours(slot(4 + 2 * u), t, 2 * e + 1)
+            diff = ring.tile([P, V], F32)
+            gain = ring.tile([P, V], F32)
+            nc.gpsimd.tensor_tensor(diff[:], slot(4 + 2 * u), slot(4 + 2 * u + 1), SUB)
+            nc.scalar.activation(gain[:], diff[:], RELU)
+            gains.append(gain)
+            if u > 0:
+                add_gain(u - 1)
+        add_gain(len(units) - 1)
         for d in range(4):
-            gather_neighbours(slot(2, d), 2, d)
-        gather_neighbours(slot(last, 0), last, 0)
-        gather_neighbours(slot(last, 3), last, 1)
-        nc.vector.tensor_tensor(pairs[:, :, 2, :], slot(2, 0, 2).rearrange("p (e v) -> p e v", e=2), slot(2, 2, 2).rearrange("p (e v) -> p e v", e=2), MAX)
-        gather_neighbours(slot(last, 2), last, 2)
-        nc.vector.tensor_tensor(slot(last, 1), slot(last, 0), slot(last, 3), MAX)
-        gather_neighbours(pairs[:, 1, last, :], last, 3)
-        nc.vector.tensor_tensor(pairs[:, 0, last, :], slot(last, 1), slot(last, 2), MAX)
+            gather_neighbours(slot(d), last, d)
+        for e in range(2):
+            nc.vector.tensor_tensor(pairs[:, e, last, :], slot(2 * e), slot(2 * e + 1), MAX)
+
+        w23_bf = slot(12, 2).rearrange("p (a n j) -> p a n j", a=2, j=PACK)
+        for a in range(2):
+            nc.scalar.copy(w23_bf[:, a].rearrange("p (c i) j -> p c j i", i=4), w23_raw[a][:].rearrange("p j (c i) -> p c j i", i=4))
+        w23_cd = keep.tile([P, 2 * N], U32, align_bytes=64)
+        w23_sc = keep.tile([P, 2 * N], U8, align_bytes=64)
+        nc.vector.quantize_mx(out=w23_cd[:].bitcast(FP8X4), scales=w23_sc[:], in_=slot(12, 2))
+        nc.vector.tensor_tensor(z_planes[:], pairs[:, 0], pairs[:, 1], MAX)
 
         def interleave(dst, planes):
             nc.scalar.copy(dst.rearrange("p (c i) t -> p c t i", i=4), planes.rearrange("p t (c i) -> p c t i", i=4))
@@ -141,8 +140,6 @@ def tile_picked_sagecat_max_p_kernel(tc, x_words, x_scales, w1, w2, w3, offs, ce
             planes = home.rearrange("p (t v) -> p t v", t=PACK)
             for t in range(PACK):
                 nc.vector.tensor_copy(planes[:, t, :], h[t][:].indirect(cen_sb[:, v0 // 16 : v1 // 16]))
-                if v0 == 0 and t == 0:
-                    nc.vector.tensor_tensor(z_planes[:], pairs[:, 0], pairs[:, 1], MAX)
             return planes
 
         def open_group(v0, v1):

@@ -63,26 +63,30 @@ def tile_picked_sagecat_max_p_kernel(tc, x_words, x_scales, w1, w2, w3, offs, ce
         x_cd = keep.tile([P, S], U32, align_bytes=64)
         nc.vector.tensor_copy(x_cd[:], table_words[:].indirect(offs_sb[:]))
 
-        w1_rest = keep.tile([P, PACK - 1, P, PACK], BF16, align_bytes=64)
-        w1_first = w1_rest[:, 0]
+        w1_bf = keep.tile([P, PACK - 1, P, PACK], BF16, align_bytes=64)
         dealt = w1_raw[:].rearrange("p j (m t) -> p m j t", t=PACK)
-        nc.scalar.copy(w1_first[:, :SCALAR_SHARE, :], dealt[:, :SCALAR_SHARE, :, 0])
-        nc.vector.tensor_copy(w1_first[:, SCALAR_SHARE:, :], dealt[:, SCALAR_SHARE:, :, 0])
-        w1_bf = [w1_first] + [w1_rest[:, t] for t in range(PACK - 1)]
+        w1_cd = keep.tile([P, H], U32, align_bytes=64)
+        w1_sc = keep.tile([P, H], U8, align_bytes=64)
+
+        def quantise_w1(t0, t1, src):
+            nc.vector.quantize_mx(out=w1_cd[:, t0 * P : t1 * P].bitcast(FP8X4), scales=w1_sc[:, t0 * P : t1 * P], in_=src.rearrange("p t m j -> p (t m j)"))
+
+        nc.scalar.copy(w1_bf[:, 1, :SCALAR_SHARE, :], dealt[:, :SCALAR_SHARE, :, 0])
+        nc.vector.tensor_copy(w1_bf[:, 1, SCALAR_SHARE:, :], dealt[:, SCALAR_SHARE:, :, 0])
+        quantise_w1(0, 1, w1_bf[:, 1:2])
+        nc.scalar.copy(w1_bf[:, 0], dealt[:, :, :, 1])
+        nc.vector.tensor_copy(w1_bf[:, 1:].rearrange("p t m j -> p m j t"), dealt[:, :, :, 2:])
+        quantise_w1(1, 2, w1_bf[:, 0:1])
+        quantise_w1(2, 4, w1_bf[:, 1:])
 
         h = []
         for t in range(PACK):
-            w1_cd = keep.tile([P, P], U32, align_bytes=64, name="w1_cd%d" % t)
-            w1_sc = keep.tile([P, P], U8, align_bytes=64, name="w1_sc%d" % t)
-            nc.vector.quantize_mx(out=w1_cd[:].bitcast(FP8X4), scales=w1_sc[:], in_=w1_bf[t].rearrange("p m j -> p (m j)"))
-            if t == 0:
-                nc.vector.tensor_copy(w1_rest[:].rearrange("p t m j -> p m j t"), dealt[:, :, :, 1:])
             ht = keep.tile([P, S], F32, name="h%d" % t)
             step = BANK // 2 if t == 0 else BANK
             for s0 in range(0, S, step):
                 nodes = slice(s0, s0 + step)
                 acc = psum_h.tile([P, BANK], F32)
-                nc.tensor.matmul_mx(out=acc[:, :step], lhsT=w1_cd[:].bitcast(FP8X4), lhsT_scale=w1_sc[:],
+                nc.tensor.matmul_mx(out=acc[:, :step], lhsT=w1_cd[:, t * P : (t + 1) * P].bitcast(FP8X4), lhsT_scale=w1_sc[:, t * P : (t + 1) * P],
                                     rhs=x_cd[:, nodes].bitcast(FP8X4), rhs_scale=x_sc[:, nodes], start=True, stop=True)
                 nc.scalar.activation(ht[:, nodes], acc[:, :step], RELU)
             h.append(ht)
@@ -99,18 +103,26 @@ def tile_picked_sagecat_max_p_kernel(tc, x_words, x_scales, w1, w2, w3, offs, ce
             nc.vector.tensor_copy(dst, h[t][:].indirect(pos_sb[d][:]))
 
         units = [(t, e) for t in range(last) for e in range(2)]
+        first_home = [slot(4 + u) for u in range(len(units))]
+        first_home[3] = slot(13)
+        first_home[4] = slot(14)
+        first_home[5] = pairs[:, 0, last, :]
+        second_home = [slot(s) for s in range(7, 13)]
         gains = []
 
         def add_gain(u):
             t, e = units[u]
-            nc.gpsimd.tensor_tensor(pairs[:, e, t, :], slot(4 + 2 * u + 1), gains[u][:], ADD)
+            nc.gpsimd.tensor_tensor(pairs[:, e, t, :], first_home[u], gains[u][:], ADD)
 
         for u, (t, e) in enumerate(units):
-            gather_neighbours(slot(4 + 2 * u + 1), t, 2 * e)
-            gather_neighbours(slot(4 + 2 * u), t, 2 * e + 1)
+            gather_neighbours(first_home[u], t, 2 * e)
+            gather_neighbours(second_home[u], t, 2 * e + 1)
             diff = ring.tile([P, V], F32)
-            gain = ring.tile([P, V], F32)
-            nc.gpsimd.tensor_tensor(diff[:], slot(4 + 2 * u), slot(4 + 2 * u + 1), SUB)
+            if u == len(units) - 1:
+                gain = keep.tile([P, V], F32, align_bytes=64, tag="late", name="last_gain")
+            else:
+                gain = ring.tile([P, V], F32)
+            nc.gpsimd.tensor_tensor(diff[:], second_home[u], first_home[u], SUB)
             nc.scalar.activation(gain[:], diff[:], RELU)
             gains.append(gain)
             if u > 0:
@@ -118,16 +130,24 @@ def tile_picked_sagecat_max_p_kernel(tc, x_words, x_scales, w1, w2, w3, offs, ce
         add_gain(len(units) - 1)
         for d in range(4):
             gather_neighbours(slot(d), last, d)
-        for e in range(2):
-            nc.vector.tensor_tensor(pairs[:, e, last, :], slot(2 * e), slot(2 * e + 1), MAX)
 
-        w23_bf = slot(12, 2).rearrange("p (a n j) -> p a n j", a=2, j=PACK)
+        (a0, a1), (b0, b1) = GATHER_PIECES
+        planes_a = slot(13, PACK).rearrange("p (t v) -> p t v", t=PACK)[:, :, a0:a1]
+
+        def gather_centres(planes, t, v0, v1):
+            nc.vector.tensor_copy(planes[:, t, :], h[t][:].indirect(cen_sb[:, v0 // 16 : v1 // 16]))
+
+        gather_centres(planes_a, 0, a0, a1)
+        nc.vector.tensor_tensor(pairs[:, :, last, :], slot(0, 2).rearrange("p (e v) -> p e v", e=2), slot(2, 2).rearrange("p (e v) -> p e v", e=2), MAX)
+        w23_bf = slot(14, 2).rearrange("p (a n j) -> p a n j", a=2, j=PACK)
         for a in range(2):
             nc.scalar.copy(w23_bf[:, a].rearrange("p (c i) j -> p c j i", i=4), w23_raw[a][:].rearrange("p j (c i) -> p c j i", i=4))
-        w23_cd = keep.tile([P, 2 * N], U32, align_bytes=64)
+        w23_cd = keep.tile([P, 2 * N], U32, align_bytes=64, tag="late")
         w23_sc = keep.tile([P, 2 * N], U8, align_bytes=64)
-        nc.vector.quantize_mx(out=w23_cd[:].bitcast(FP8X4), scales=w23_sc[:], in_=slot(12, 2))
+        nc.vector.quantize_mx(out=w23_cd[:].bitcast(FP8X4), scales=w23_sc[:], in_=slot(14, 2))
         nc.vector.tensor_tensor(z_planes[:], pairs[:, 0], pairs[:, 1], MAX)
+        for t in range(1, PACK):
+            gather_centres(planes_a, t, a0, a1)
 
         def interleave(dst, planes):
             nc.scalar.copy(dst.rearrange("p (c i) t -> p c t i", i=4), planes.rearrange("p t (c i) -> p c t i", i=4))
@@ -135,12 +155,6 @@ def tile_picked_sagecat_max_p_kernel(tc, x_words, x_scales, w1, w2, w3, offs, ce
         z_bf = keep.tile([P, V, PACK], BF16, align_bytes=64)
         z_cd = keep.tile([P, V], U32, align_bytes=64)
         z_sc = keep.tile([P, V], U8, align_bytes=64)
-
-        def gather_centres(v0, v1, home):
-            planes = home.rearrange("p (t v) -> p t v", t=PACK)
-            for t in range(PACK):
-                nc.vector.tensor_copy(planes[:, t, :], h[t][:].indirect(cen_sb[:, v0 // 16 : v1 // 16]))
-            return planes
 
         def open_group(v0, v1):
             acc_o = psum_o.tile([P, BANK], F32)
@@ -158,15 +172,15 @@ def tile_picked_sagecat_max_p_kernel(tc, x_words, x_scales, w1, w2, w3, offs, ce
             engine_copy(res[:], acc_o[:, : v1 - v0])
             nc.sync.dma_start(out[:, v0:v1], res[:])
 
-        (a0, a1), (b0, b1) = GATHER_PIECES
-        planes_a = gather_centres(a0, a1, nb[:, 16 * V - a1 : 16 * V + last * a1])
         interleave(z_bf[:], z_planes[:])
         nc.vector.quantize_mx(out=z_cd[:].bitcast(FP8X4), scales=z_sc[:], in_=z_bf[:].rearrange("p v t -> p (v t)"))
         accs = [open_group(v0, v1) for v0, v1 in PIECES]
         c_bfs = [keep.tile([P, v1 - v0, PACK], BF16, align_bytes=64, name="c_bf%d" % v0) for v0, v1 in PIECES]
         for (v0, v1), c_bf in zip(PIECES[:-1], c_bfs):
             interleave(c_bf[:], planes_a[:, :, v0:v1])
-        planes_b = gather_centres(b0, b1, z_bf[:, : b1 - b0, :].rearrange("p v t -> p (v t)"))
+        planes_b = z_bf[:, : b1 - b0, :].rearrange("p v t -> p (v t)").rearrange("p (t v) -> p t v", t=PACK)
+        for t in range(PACK):
+            gather_centres(planes_b, t, b0, b1)
         interleave(c_bfs[-1][:], planes_b)
         for (v0, v1), acc_o, c_bf, engine_copy in zip(PIECES, accs, c_bfs, (nc.scalar.copy, nc.scalar.copy, nc.vector.tensor_copy)):
             close_group(v0, v1, acc_o, c_bf, engine_copy)

@@ -19,19 +19,34 @@ RELU = mybir.ActivationFunctionType.Relu
 
 P = 128
 PACK = 4
+DEGREE = 4
 BANK = 512
+LIST_COLUMN = 16
+QUADRANT = 32
+RUN = 4
 SCALAR_SHARE = 80
-GATHER_PIECES = ((0, 384), (384, 512))
-PIECES = ((0, 256), (256, 384), (384, 512))
+FIRST_TILE_CUTS = (0, 256, 512, 768, 896, S)
+WIDE_END = 384
+PIECES = ((0, 256), (256, WIDE_END), (WIDE_END, V))
+
+LAST_TILE_SLOTS = 0
+BASE_SLOTS = 4
+OTHER_SLOTS = 7
+CENTRE_SLOTS = 13
+W23_SLOTS = 14
+PAIR_SLOTS = 16
+SLOTS = 24
 
 
-def tile_picked_sagecat_max_p_kernel(tc, x_words, x_scales, w1, w2, w3, offs, cen, pos1, pos2, pos3, pos4, out):
+def tile_picked_sagecat_max_p_kernel(
+    tc, x_words, x_scales, w1, w2, w3, offs, cen, pos1, pos2, pos3, pos4, out
+):
     nc = tc.nc
     with ExitStack() as ctx:
         keep = ctx.enter_context(tc.tile_pool(name="keep", bufs=1))
         ring = ctx.enter_context(tc.tile_pool(name="ring", bufs=2))
-        psum_h = ctx.enter_context(tc.psum_pool(name="psum_h", bufs=4))
-        psum_o = ctx.enter_context(tc.psum_pool(name="psum_o", bufs=3))
+        psum_h = ctx.enter_context(tc.psum_pool(name="psum_h", bufs=len(FIRST_TILE_CUTS) - 1))
+        psum_o = ctx.enter_context(tc.psum_pool(name="psum_o", bufs=len(PIECES)))
 
         def load_list(src, name):
             tile = keep.tile(list(src.shape), U16, name=name)
@@ -42,8 +57,11 @@ def tile_picked_sagecat_max_p_kernel(tc, x_words, x_scales, w1, w2, w3, offs, ce
         nc.vector.memset(table_scales[:].bitcast(I32), 0)
         offs_sb = load_list(offs, "offs_sb")
         pos_sb = [load_list(pos1, "pos1_sb")]
-        for q in range(4):
-            nc.sync.dma_start(table_scales[32 * q : 32 * q + 4, :].bitcast(I32), x_scales[0, 4 * q : 4 * q + 4, :].bitcast(I32))
+        for q in range(P // QUADRANT):
+            nc.sync.dma_start(
+                table_scales[QUADRANT * q : QUADRANT * q + 4, :].bitcast(I32),
+                x_scales[0, 4 * q : 4 * q + 4, :].bitcast(I32),
+            )
         table_words = keep.tile([P, T], U32, align_bytes=64)
         nc.sync.dma_start(table_words[:].bitcast(I32), x_words[0].rearrange("p c r -> p (c r)").bitcast(I32))
         w1_raw = keep.tile([P, PACK, H], F32)
@@ -69,7 +87,11 @@ def tile_picked_sagecat_max_p_kernel(tc, x_words, x_scales, w1, w2, w3, offs, ce
         w1_sc = keep.tile([P, H], U8, align_bytes=64)
 
         def quantise_w1(t0, t1, src):
-            nc.vector.quantize_mx(out=w1_cd[:, t0 * P : t1 * P].bitcast(FP8X4), scales=w1_sc[:, t0 * P : t1 * P], in_=src.rearrange("p t m j -> p (t m j)"))
+            nc.vector.quantize_mx(
+                out=w1_cd[:, t0 * P : t1 * P].bitcast(FP8X4),
+                scales=w1_sc[:, t0 * P : t1 * P],
+                in_=src.rearrange("p t m j -> p (t m j)"),
+            )
 
         nc.scalar.copy(w1_bf[:, 1, :SCALAR_SHARE, :], dealt[:, :SCALAR_SHARE, :, 0])
         nc.vector.tensor_copy(w1_bf[:, 1, SCALAR_SHARE:, :], dealt[:, SCALAR_SHARE:, :, 0])
@@ -82,75 +104,89 @@ def tile_picked_sagecat_max_p_kernel(tc, x_words, x_scales, w1, w2, w3, offs, ce
         h = []
         for t in range(PACK):
             ht = keep.tile([P, S], F32, name="h%d" % t)
-            step = BANK // 2 if t == 0 else BANK
-            for s0 in range(0, S, step):
-                nodes = slice(s0, s0 + step)
+            cuts = FIRST_TILE_CUTS if t == 0 else (0, BANK, S)
+            for s0, s1 in zip(cuts, cuts[1:]):
                 acc = psum_h.tile([P, BANK], F32)
-                nc.tensor.matmul_mx(out=acc[:, :step], lhsT=w1_cd[:, t * P : (t + 1) * P].bitcast(FP8X4), lhsT_scale=w1_sc[:, t * P : (t + 1) * P],
-                                    rhs=x_cd[:, nodes].bitcast(FP8X4), rhs_scale=x_sc[:, nodes], start=True, stop=True)
-                nc.scalar.activation(ht[:, nodes], acc[:, :step], RELU)
+                nc.tensor.matmul_mx(
+                    out=acc[:, : s1 - s0],
+                    lhsT=w1_cd[:, t * P : (t + 1) * P].bitcast(FP8X4),
+                    lhsT_scale=w1_sc[:, t * P : (t + 1) * P],
+                    rhs=x_cd[:, s0:s1].bitcast(FP8X4),
+                    rhs_scale=x_sc[:, s0:s1],
+                    start=True,
+                    stop=True,
+                )
+                if t == 0 and s0 == FIRST_TILE_CUTS[2]:
+                    nc.vector.tensor_scalar_max(ht[:, s0:s1], acc[:, : s1 - s0], 0.0)
+                else:
+                    nc.scalar.activation(ht[:, s0:s1], acc[:, : s1 - s0], RELU)
             h.append(ht)
 
         last = PACK - 1
         z_planes = keep.tile([P, PACK, V], BF16)
-        nb = keep.tile([P, PACK * 6 * V], BF16, align_bytes=64)
-        pairs = nb[:, PACK * 4 * V :].rearrange("p (e t v) -> p e t v", e=2, t=PACK)
+        nb = keep.tile([P, SLOTS * V], BF16, align_bytes=64)
 
         def slot(s, count=1):
             return nb[:, s * V : (s + count) * V]
 
+        pairs = slot(PAIR_SLOTS, 2 * PACK).rearrange("p (e t v) -> p e t v", e=2, t=PACK)
+
         def gather_neighbours(dst, t, d):
             nc.vector.tensor_copy(dst, h[t][:].indirect(pos_sb[d][:]))
 
-        units = [(t, e) for t in range(last) for e in range(2)]
-        first_home = [slot(4 + u) for u in range(len(units))]
-        first_home[3] = slot(13)
-        first_home[4] = slot(14)
-        first_home[5] = pairs[:, 0, last, :]
-        second_home = [slot(s) for s in range(7, 13)]
+        maxima = [(t, e) for t in range(last) for e in range(2)]
+        bases = [slot(BASE_SLOTS + u) for u in range(3)] + [slot(CENTRE_SLOTS), slot(W23_SLOTS), pairs[:, 0, last, :]]
+        others = [slot(OTHER_SLOTS + u) for u in range(len(maxima))]
         gains = []
 
         def add_gain(u):
-            t, e = units[u]
-            nc.gpsimd.tensor_tensor(pairs[:, e, t, :], first_home[u], gains[u][:], ADD)
+            t, e = maxima[u]
+            nc.gpsimd.tensor_tensor(pairs[:, e, t, :], bases[u], gains[u][:], ADD)
 
-        for u, (t, e) in enumerate(units):
-            gather_neighbours(first_home[u], t, 2 * e)
-            gather_neighbours(second_home[u], t, 2 * e + 1)
+        for u, (t, e) in enumerate(maxima):
+            gather_neighbours(bases[u], t, 2 * e)
+            gather_neighbours(others[u], t, 2 * e + 1)
             diff = ring.tile([P, V], F32)
-            if u == len(units) - 1:
+            if u == len(maxima) - 1:
                 gain = keep.tile([P, V], F32, align_bytes=64, tag="late", name="last_gain")
             else:
                 gain = ring.tile([P, V], F32)
-            nc.gpsimd.tensor_tensor(diff[:], second_home[u], first_home[u], SUB)
+            nc.gpsimd.tensor_tensor(diff[:], others[u], bases[u], SUB)
             nc.scalar.activation(gain[:], diff[:], RELU)
             gains.append(gain)
             if u > 0:
                 add_gain(u - 1)
-        add_gain(len(units) - 1)
-        for d in range(4):
-            gather_neighbours(slot(d), last, d)
+        add_gain(len(maxima) - 1)
+        for d in range(DEGREE):
+            gather_neighbours(slot(LAST_TILE_SLOTS + d), last, d)
 
-        (a0, a1), (b0, b1) = GATHER_PIECES
-        planes_a = slot(13, PACK).rearrange("p (t v) -> p t v", t=PACK)[:, :, a0:a1]
+        wide_planes = slot(CENTRE_SLOTS, PACK).rearrange("p (t v) -> p t v", t=PACK)[:, :, :WIDE_END]
 
         def gather_centres(planes, t, v0, v1):
-            nc.vector.tensor_copy(planes[:, t, :], h[t][:].indirect(cen_sb[:, v0 // 16 : v1 // 16]))
+            nc.vector.tensor_copy(planes[:, t, :], h[t][:].indirect(cen_sb[:, v0 // LIST_COLUMN : v1 // LIST_COLUMN]))
 
-        gather_centres(planes_a, 0, a0, a1)
-        nc.vector.tensor_tensor(pairs[:, :, last, :], slot(0, 2).rearrange("p (e v) -> p e v", e=2), slot(2, 2).rearrange("p (e v) -> p e v", e=2), MAX)
-        w23_bf = slot(14, 2).rearrange("p (a n j) -> p a n j", a=2, j=PACK)
+        gather_centres(wide_planes, 0, 0, WIDE_END)
+        nc.vector.tensor_tensor(
+            pairs[:, :, last, :],
+            slot(LAST_TILE_SLOTS, 2).rearrange("p (e v) -> p e v", e=2),
+            slot(LAST_TILE_SLOTS + 2, 2).rearrange("p (e v) -> p e v", e=2),
+            MAX,
+        )
+        w23_bf = slot(W23_SLOTS, 2).rearrange("p (a n j) -> p a n j", a=2, j=PACK)
         for a in range(2):
-            nc.scalar.copy(w23_bf[:, a].rearrange("p (c i) j -> p c j i", i=4), w23_raw[a][:].rearrange("p j (c i) -> p c j i", i=4))
+            nc.scalar.copy(
+                w23_bf[:, a].rearrange("p (c i) j -> p c j i", i=RUN),
+                w23_raw[a][:].rearrange("p j (c i) -> p c j i", i=RUN),
+            )
         w23_cd = keep.tile([P, 2 * N], U32, align_bytes=64, tag="late")
         w23_sc = keep.tile([P, 2 * N], U8, align_bytes=64)
-        nc.vector.quantize_mx(out=w23_cd[:].bitcast(FP8X4), scales=w23_sc[:], in_=slot(14, 2))
+        nc.vector.quantize_mx(out=w23_cd[:].bitcast(FP8X4), scales=w23_sc[:], in_=slot(W23_SLOTS, 2))
         nc.vector.tensor_tensor(z_planes[:], pairs[:, 0], pairs[:, 1], MAX)
         for t in range(1, PACK):
-            gather_centres(planes_a, t, a0, a1)
+            gather_centres(wide_planes, t, 0, WIDE_END)
 
         def interleave(dst, planes):
-            nc.scalar.copy(dst.rearrange("p (c i) t -> p c t i", i=4), planes.rearrange("p t (c i) -> p c t i", i=4))
+            nc.scalar.copy(dst.rearrange("p (c i) t -> p c t i", i=RUN), planes.rearrange("p t (c i) -> p c t i", i=RUN))
 
         z_bf = keep.tile([P, V, PACK], BF16, align_bytes=64)
         z_cd = keep.tile([P, V], U32, align_bytes=64)
@@ -158,29 +194,45 @@ def tile_picked_sagecat_max_p_kernel(tc, x_words, x_scales, w1, w2, w3, offs, ce
 
         def open_group(v0, v1):
             acc_o = psum_o.tile([P, BANK], F32)
-            nc.tensor.matmul_mx(out=acc_o[:, : v1 - v0], lhsT=w23_cd[:, :N].bitcast(FP8X4), lhsT_scale=w23_sc[:, :N],
-                                rhs=z_cd[:, v0:v1].bitcast(FP8X4), rhs_scale=z_sc[:, v0:v1], start=True, stop=False)
+            nc.tensor.matmul_mx(
+                out=acc_o[:, : v1 - v0],
+                lhsT=w23_cd[:, :N].bitcast(FP8X4),
+                lhsT_scale=w23_sc[:, :N],
+                rhs=z_cd[:, v0:v1].bitcast(FP8X4),
+                rhs_scale=z_sc[:, v0:v1],
+                start=True,
+                stop=False,
+            )
             return acc_o
 
-        def close_group(v0, v1, acc_o, c_bf, engine_copy):
+        def close_group(v0, v1, acc_o, c_bf, queue):
             c_cd = keep.tile([P, v1 - v0], U32, align_bytes=64, name="c_cd%d" % v0)
             c_sc = keep.tile([P, v1 - v0], U8, align_bytes=64, name="c_sc%d" % v0)
             nc.vector.quantize_mx(out=c_cd[:].bitcast(FP8X4), scales=c_sc[:], in_=c_bf[:].rearrange("p v t -> p (v t)"))
-            nc.tensor.matmul_mx(out=acc_o[:, : v1 - v0], lhsT=w23_cd[:, N:].bitcast(FP8X4), lhsT_scale=w23_sc[:, N:],
-                                rhs=c_cd[:].bitcast(FP8X4), rhs_scale=c_sc[:], start=False, stop=True)
+            nc.tensor.matmul_mx(
+                out=acc_o[:, : v1 - v0],
+                lhsT=w23_cd[:, N:].bitcast(FP8X4),
+                lhsT_scale=w23_sc[:, N:],
+                rhs=c_cd[:].bitcast(FP8X4),
+                rhs_scale=c_sc[:],
+                start=False,
+                stop=True,
+            )
             res = keep.tile([P, v1 - v0], F32, name="res%d" % v0)
-            engine_copy(res[:], acc_o[:, : v1 - v0])
-            nc.sync.dma_start(out[:, v0:v1], res[:])
+            nc.scalar.copy(res[:], acc_o[:, : v1 - v0])
+            queue.dma_start(out[:, v0:v1], res[:])
 
         interleave(z_bf[:], z_planes[:])
         nc.vector.quantize_mx(out=z_cd[:].bitcast(FP8X4), scales=z_sc[:], in_=z_bf[:].rearrange("p v t -> p (v t)"))
         accs = [open_group(v0, v1) for v0, v1 in PIECES]
         c_bfs = [keep.tile([P, v1 - v0, PACK], BF16, align_bytes=64, name="c_bf%d" % v0) for v0, v1 in PIECES]
         for (v0, v1), c_bf in zip(PIECES[:-1], c_bfs):
-            interleave(c_bf[:], planes_a[:, :, v0:v1])
-        planes_b = z_bf[:, : b1 - b0, :].rearrange("p v t -> p (v t)").rearrange("p (t v) -> p t v", t=PACK)
+            interleave(c_bf[:], wide_planes[:, :, v0:v1])
+
+        narrow_planes = z_bf[:, : V - WIDE_END, :].rearrange("p v t -> p (v t)").rearrange("p (t v) -> p t v", t=PACK)
         for t in range(PACK):
-            gather_centres(planes_b, t, b0, b1)
-        interleave(c_bfs[-1][:], planes_b)
-        for (v0, v1), acc_o, c_bf, engine_copy in zip(PIECES, accs, c_bfs, (nc.scalar.copy, nc.scalar.copy, nc.vector.tensor_copy)):
-            close_group(v0, v1, acc_o, c_bf, engine_copy)
+            gather_centres(narrow_planes, t, WIDE_END, V)
+        interleave(c_bfs[-1][:], narrow_planes)
+
+        for (v0, v1), acc_o, c_bf, queue in zip(PIECES, accs, c_bfs, (nc.sync, nc.sync, nc.scalar)):
+            close_group(v0, v1, acc_o, c_bf, queue)

@@ -24,8 +24,10 @@ BANK = 512
 LIST_COLUMN = 16
 QUADRANT = 32
 RUN = 4
-SCALAR_SHARE = 80
-FIRST_TILE_CUTS = (0, 256, 512, 768, 896, S)
+FRONT = 512
+LATE = 768
+FIRST_TILE_CUTS = (0, 256, 512, LATE, 896, S)
+OTHER_TILE_BANKS = [(0, BANK), (BANK, LATE, S)]
 WIDE_END = 384
 PIECES = ((0, 256), (256, WIDE_END), (WIDE_END, V))
 
@@ -54,35 +56,43 @@ def tile_picked_sagecat_max_p_kernel(
             return tile
 
         table_scales = keep.tile([P, T], U8, align_bytes=64)
-        nc.vector.memset(table_scales[:].bitcast(I32), 0)
+        nc.vector.memset(table_scales[:, : T // 2].bitcast(I32), 0)
+        nc.gpsimd.memset(table_scales[:, T // 2 :].bitcast(I32), 0)
         offs_sb = load_list(offs, "offs_sb")
-        pos_sb = [load_list(pos1, "pos1_sb")]
+        table_words = keep.tile([P, T], U32, align_bytes=64)
+        words_hbm = x_words[0].rearrange("p c r -> p (c r)").bitcast(I32)
+        nc.sync.dma_start(table_words[:, :FRONT].bitcast(I32), words_hbm[:, :FRONT])
         for q in range(P // QUADRANT):
-            nc.sync.dma_start(
+            (nc.sync, nc.scalar)[q % 2].dma_start(
                 table_scales[QUADRANT * q : QUADRANT * q + 4, :].bitcast(I32),
                 x_scales[0, 4 * q : 4 * q + 4, :].bitcast(I32),
             )
-        table_words = keep.tile([P, T], U32, align_bytes=64)
-        nc.sync.dma_start(table_words[:].bitcast(I32), x_words[0].rearrange("p c r -> p (c r)").bitcast(I32))
+        nc.sync.dma_start(table_words[:, FRONT:].bitcast(I32), words_hbm[:, FRONT:])
         w1_raw = keep.tile([P, PACK, H], F32)
         nc.sync.dma_start(w1_raw[:], w1.rearrange("(p j) c -> p j c", j=PACK))
+        pos_sb = [load_list(pos1, "pos1_sb")]
         pos_sb.append(load_list(pos2, "pos2_sb"))
         pos_sb.append(load_list(pos3, "pos3_sb"))
         pos_sb.append(load_list(pos4, "pos4_sb"))
         w23_raw = []
         for a, w in enumerate((w3, w2)):
             raw = keep.tile([P, PACK, N], F32, name="w23_raw%d" % a)
-            nc.sync.dma_start(raw[:], w.rearrange("(p j) n -> p j n", j=PACK))
+            rows = w.rearrange("(a t b) n -> b a t n", t=PACK, b=RUN)
+            for b in range(RUN):
+                nc.sync.dma_start(raw[b:P:RUN], rows[b])
             w23_raw.append(raw)
         cen_sb = load_list(cen, "cen_sb")
 
         x_sc = keep.tile([P, S], U8, align_bytes=64)
         nc.vector.tensor_copy(x_sc[:], table_scales[:].indirect(offs_sb[:]))
-        x_cd = keep.tile([P, S], U32, align_bytes=64)
-        nc.vector.tensor_copy(x_cd[:], table_words[:].indirect(offs_sb[:]))
+        x_cd = keep.tile([P, LATE], U32, align_bytes=64)
+        nc.vector.tensor_copy(x_cd[:], table_words[:].indirect(offs_sb[:, : LATE // LIST_COLUMN]))
 
-        w1_bf = keep.tile([P, PACK - 1, P, PACK], BF16, align_bytes=64)
-        dealt = w1_raw[:].rearrange("p j (m t) -> p m j t", t=PACK)
+        dealt = w1_raw[:].rearrange("p j (a t b) -> p t a j b", t=PACK, b=RUN)
+
+        def cast_view(tile):
+            return tile[:].rearrange("p t (a b) j -> p t a j b", b=RUN)
+
         w1_cd = keep.tile([P, H], U32, align_bytes=64)
         w1_sc = keep.tile([P, H], U8, align_bytes=64)
 
@@ -93,33 +103,36 @@ def tile_picked_sagecat_max_p_kernel(
                 in_=src.rearrange("p t m j -> p (t m j)"),
             )
 
-        nc.scalar.copy(w1_bf[:, 1, :SCALAR_SHARE, :], dealt[:, :SCALAR_SHARE, :, 0])
-        nc.vector.tensor_copy(w1_bf[:, 1, SCALAR_SHARE:, :], dealt[:, SCALAR_SHARE:, :, 0])
-        quantise_w1(0, 1, w1_bf[:, 1:2])
-        nc.scalar.copy(w1_bf[:, 0], dealt[:, :, :, 1])
-        nc.vector.tensor_copy(w1_bf[:, 1:].rearrange("p t m j -> p m j t"), dealt[:, :, :, 2:])
-        quantise_w1(1, 2, w1_bf[:, 0:1])
-        quantise_w1(2, 4, w1_bf[:, 1:])
+        w1_bf0 = keep.tile([P, 1, P, PACK], BF16, align_bytes=64, tag="first")
+        w1_bf1 = keep.tile([P, 1, P, PACK], BF16, align_bytes=64)
+        w1_bf23 = keep.tile([P, 2, P, PACK], BF16, align_bytes=64)
+        nc.scalar.copy(cast_view(w1_bf0)[:, 0], dealt[:, 0])
+        nc.vector.tensor_copy(cast_view(w1_bf23)[:, 1], dealt[:, 3])
+        quantise_w1(0, 1, w1_bf0[:])
+        x_late = keep.tile([P, S - LATE], U32, align_bytes=64, tag="first")
+        nc.vector.tensor_copy(x_late[:], table_words[:].indirect(offs_sb[:, LATE // LIST_COLUMN :]))
+        nc.scalar.copy(cast_view(w1_bf1)[:, 0], dealt[:, 1])
+        nc.scalar.copy(cast_view(w1_bf23)[:, 0], dealt[:, 2])
+        quantise_w1(1, 2, w1_bf1[:])
+        quantise_w1(2, 4, w1_bf23[:])
 
         h = []
         for t in range(PACK):
             ht = keep.tile([P, S], F32, name="h%d" % t)
-            cuts = FIRST_TILE_CUTS if t == 0 else (0, BANK, S)
-            for s0, s1 in zip(cuts, cuts[1:]):
+            banks = [(s0, s1) for s0, s1 in zip(FIRST_TILE_CUTS, FIRST_TILE_CUTS[1:])] if t == 0 else OTHER_TILE_BANKS
+            for cuts in banks:
                 acc = psum_h.tile([P, BANK], F32)
-                nc.tensor.matmul_mx(
-                    out=acc[:, : s1 - s0],
-                    lhsT=w1_cd[:, t * P : (t + 1) * P].bitcast(FP8X4),
-                    lhsT_scale=w1_sc[:, t * P : (t + 1) * P],
-                    rhs=x_cd[:, s0:s1].bitcast(FP8X4),
-                    rhs_scale=x_sc[:, s0:s1],
-                    start=True,
-                    stop=True,
-                )
-                if t == 0 and s0 == FIRST_TILE_CUTS[2]:
-                    nc.vector.tensor_scalar_max(ht[:, s0:s1], acc[:, : s1 - s0], 0.0)
-                else:
-                    nc.scalar.activation(ht[:, s0:s1], acc[:, : s1 - s0], RELU)
+                for s0, s1 in zip(cuts, cuts[1:]):
+                    nc.tensor.matmul_mx(
+                        out=acc[:, s0 - cuts[0] : s1 - cuts[0]],
+                        lhsT=w1_cd[:, t * P : (t + 1) * P].bitcast(FP8X4),
+                        lhsT_scale=w1_sc[:, t * P : (t + 1) * P],
+                        rhs=(x_cd[:, s0:s1] if s1 <= LATE else x_late[:, s0 - LATE : s1 - LATE]).bitcast(FP8X4),
+                        rhs_scale=x_sc[:, s0:s1],
+                        start=True,
+                        stop=True,
+                    )
+                nc.scalar.activation(ht[:, cuts[0] : cuts[-1]], acc[:, : cuts[-1] - cuts[0]], RELU)
             h.append(ht)
 
         last = PACK - 1

@@ -24,7 +24,6 @@ BANK = 512
 LIST_COLUMN = 16
 QUADRANT = 32
 RUN = 4
-FRONT = 512
 LATE = 768
 FIRST_TILE_CUTS = (0, 256, 512, LATE, 896, S)
 OTHER_TILE_BANKS = [(0, BANK), (BANK, LATE, S)]
@@ -56,21 +55,18 @@ def tile_picked_sagecat_max_p_kernel(
             return tile
 
         table_scales = keep.tile([P, T], U8, align_bytes=64)
-        nc.vector.memset(table_scales[:, : T // 2].bitcast(I32), 0)
-        nc.gpsimd.memset(table_scales[:, T // 2 :].bitcast(I32), 0)
+        nc.vector.memset(table_scales[:].bitcast(I32), 0)
         offs_sb = load_list(offs, "offs_sb")
-        table_words = keep.tile([P, T], U32, align_bytes=64)
-        words_hbm = x_words[0].rearrange("p c r -> p (c r)").bitcast(I32)
-        nc.sync.dma_start(table_words[:, :FRONT].bitcast(I32), words_hbm[:, :FRONT])
+        pos_sb = [load_list(pos1, "pos1_sb")]
         for q in range(P // QUADRANT):
-            (nc.sync, nc.scalar)[q % 2].dma_start(
+            nc.sync.dma_start(
                 table_scales[QUADRANT * q : QUADRANT * q + 4, :].bitcast(I32),
                 x_scales[0, 4 * q : 4 * q + 4, :].bitcast(I32),
             )
-        nc.sync.dma_start(table_words[:, FRONT:].bitcast(I32), words_hbm[:, FRONT:])
+        table_words = keep.tile([P, T], U32, align_bytes=64)
+        nc.sync.dma_start(table_words[:].bitcast(I32), x_words[0].rearrange("p c r -> p (c r)").bitcast(I32))
         w1_raw = keep.tile([P, PACK, H], F32)
         nc.sync.dma_start(w1_raw[:], w1.rearrange("(p j) c -> p j c", j=PACK))
-        pos_sb = [load_list(pos1, "pos1_sb")]
         pos_sb.append(load_list(pos2, "pos2_sb"))
         pos_sb.append(load_list(pos3, "pos3_sb"))
         pos_sb.append(load_list(pos4, "pos4_sb"))

@@ -23,8 +23,10 @@ DEGREE = 4
 BANK = 512
 LIST_COLUMN = 16
 QUADRANT = 32
+SCALE_ROWS = 4
 RUN = 4
 LATE = 768
+SCALAR_SHARE = 20
 FIRST_TILE_CUTS = (0, 256, 512, LATE, 896, S)
 OTHER_TILE_BANKS = [(0, BANK), (BANK, LATE, S)]
 WIDE_END = 384
@@ -58,11 +60,8 @@ def tile_picked_sagecat_max_p_kernel(
         nc.vector.memset(table_scales[:].bitcast(I32), 0)
         offs_sb = load_list(offs, "offs_sb")
         pos_sb = [load_list(pos1, "pos1_sb")]
-        for q in range(P // QUADRANT):
-            nc.sync.dma_start(
-                table_scales[QUADRANT * q : QUADRANT * q + 4, :].bitcast(I32),
-                x_scales[0, 4 * q : 4 * q + 4, :].bitcast(I32),
-            )
+        for r in range(SCALE_ROWS):
+            nc.sync.dma_start(table_scales[r:P:QUADRANT, :].bitcast(I32), x_scales[0, r::SCALE_ROWS, :].bitcast(I32))
         table_words = keep.tile([P, T], U32, align_bytes=64)
         nc.sync.dma_start(table_words[:].bitcast(I32), x_words[0].rearrange("p c r -> p (c r)").bitcast(I32))
         w1_raw = keep.tile([P, PACK, H], F32)
@@ -102,7 +101,8 @@ def tile_picked_sagecat_max_p_kernel(
         w1_bf0 = keep.tile([P, 1, P, PACK], BF16, align_bytes=64, tag="first")
         w1_bf1 = keep.tile([P, 1, P, PACK], BF16, align_bytes=64)
         w1_bf23 = keep.tile([P, 2, P, PACK], BF16, align_bytes=64)
-        nc.scalar.copy(cast_view(w1_bf0)[:, 0], dealt[:, 0])
+        nc.scalar.copy(cast_view(w1_bf0)[:, 0, :SCALAR_SHARE], dealt[:, 0, :SCALAR_SHARE])
+        nc.vector.tensor_copy(cast_view(w1_bf0)[:, 0, SCALAR_SHARE:], dealt[:, 0, SCALAR_SHARE:])
         nc.vector.tensor_copy(cast_view(w1_bf23)[:, 1], dealt[:, 3])
         quantise_w1(0, 1, w1_bf0[:])
         x_late = keep.tile([P, S - LATE], U32, align_bytes=64, tag="first")

@@ -26,7 +26,7 @@ QUADRANT = 32
 SCALE_ROWS = 4
 RUN = 4
 LATE = 768
-SCALAR_SHARE = 20
+SCALAR_SHARE = 12
 FIRST_TILE_CUTS = (0, 256, 512, LATE, 896, S)
 OTHER_TILE_BANKS = [(0, BANK), (BANK, LATE, S)]
 WIDE_END = 384
@@ -103,14 +103,14 @@ def tile_picked_sagecat_max_p_kernel(
         w1_bf23 = keep.tile([P, 2, P, PACK], BF16, align_bytes=64)
         nc.scalar.copy(cast_view(w1_bf0)[:, 0, :SCALAR_SHARE], dealt[:, 0, :SCALAR_SHARE])
         nc.vector.tensor_copy(cast_view(w1_bf0)[:, 0, SCALAR_SHARE:], dealt[:, 0, SCALAR_SHARE:])
-        nc.vector.tensor_copy(cast_view(w1_bf23)[:, 1], dealt[:, 3])
+        nc.vector.tensor_copy(cast_view(w1_bf23)[:, 1, :16], dealt[:, 3, :16])
         quantise_w1(0, 1, w1_bf0[:])
         x_late = keep.tile([P, S - LATE], U32, align_bytes=64, tag="first")
         nc.vector.tensor_copy(x_late[:], table_words[:].indirect(offs_sb[:, LATE // LIST_COLUMN :]))
         nc.scalar.copy(cast_view(w1_bf1)[:, 0], dealt[:, 1])
         nc.scalar.copy(cast_view(w1_bf23)[:, 0], dealt[:, 2])
+        nc.scalar.copy(cast_view(w1_bf23)[:, 1, 16:], dealt[:, 3, 16:])
         quantise_w1(1, 2, w1_bf1[:])
-        quantise_w1(2, 4, w1_bf23[:])
 
         h = []
         for t in range(PACK):
@@ -128,7 +128,12 @@ def tile_picked_sagecat_max_p_kernel(
                         start=True,
                         stop=True,
                     )
-                nc.scalar.activation(ht[:, cuts[0] : cuts[-1]], acc[:, : cuts[-1] - cuts[0]], RELU)
+                if t == 0 and cuts[0] == FIRST_TILE_CUTS[2]:
+                    nc.vector.tensor_scalar_max(ht[:, cuts[0] : cuts[-1]], acc[:, : cuts[-1] - cuts[0]], 0.0)
+                else:
+                    nc.scalar.activation(ht[:, cuts[0] : cuts[-1]], acc[:, : cuts[-1] - cuts[0]], RELU)
+            if t == 0:
+                quantise_w1(2, 4, w1_bf23[:])
             h.append(ht)
 
         last = PACK - 1
@@ -190,7 +195,9 @@ def tile_picked_sagecat_max_p_kernel(
         w23_cd = keep.tile([P, 2 * N], U32, align_bytes=64, tag="late")
         w23_sc = keep.tile([P, 2 * N], U8, align_bytes=64)
         nc.vector.quantize_mx(out=w23_cd[:].bitcast(FP8X4), scales=w23_sc[:], in_=slot(W23_SLOTS, 2))
-        nc.vector.tensor_tensor(z_planes[:], pairs[:, 0], pairs[:, 1], MAX)
+        halves = (slice(0, V // 2), slice(V // 2, V))
+        for half in halves:
+            nc.vector.tensor_tensor(z_planes[:, :, half], pairs[:, 0, :, half], pairs[:, 1, :, half], MAX)
         for t in range(1, PACK):
             gather_centres(wide_planes, t, 0, WIDE_END)
 
@@ -231,17 +238,20 @@ def tile_picked_sagecat_max_p_kernel(
             nc.scalar.copy(res[:], acc_o[:, : v1 - v0])
             queue.dma_start(out[:, v0:v1], res[:])
 
-        interleave(z_bf[:], z_planes[:])
+        for half in halves:
+            interleave(z_bf[:, half], z_planes[:, :, half])
         nc.vector.quantize_mx(out=z_cd[:].bitcast(FP8X4), scales=z_sc[:], in_=z_bf[:].rearrange("p v t -> p (v t)"))
         accs = [open_group(v0, v1) for v0, v1 in PIECES]
         c_bfs = [keep.tile([P, v1 - v0, PACK], BF16, align_bytes=64, name="c_bf%d" % v0) for v0, v1 in PIECES]
         for (v0, v1), c_bf in zip(PIECES[:-1], c_bfs):
             interleave(c_bf[:], wide_planes[:, :, v0:v1])
 
-        narrow_planes = z_bf[:, : V - WIDE_END, :].rearrange("p v t -> p (v t)").rearrange("p (t v) -> p t v", t=PACK)
+        narrow_planes = z_planes[:, :, WIDE_END:]
         for t in range(PACK):
             gather_centres(narrow_planes, t, WIDE_END, V)
-        interleave(c_bfs[-1][:], narrow_planes)
+        nc.vector.tensor_copy(
+            c_bfs[-1][:].rearrange("p (c i) t -> p c t i", i=RUN), narrow_planes.rearrange("p t (c i) -> p c t i", i=RUN)
+        )
 
         for (v0, v1), acc_o, c_bf, queue in zip(PIECES, accs, c_bfs, (nc.sync, nc.sync, nc.scalar)):
             close_group(v0, v1, acc_o, c_bf, queue)

@@ -25,6 +25,7 @@ LIST_COLUMN = 16
 QUADRANT = 32
 SCALE_ROWS = 4
 RUN = 4
+LINE = 8
 LATE = 768
 SCALAR_SHARE = 12
 FIRST_TILE_CUTS = (0, 256, 512, LATE, 896, S)
@@ -202,7 +203,7 @@ def tile_picked_sagecat_max_p_kernel(
             gather_centres(wide_planes, t, 0, WIDE_END)
 
         def interleave(dst, planes):
-            nc.scalar.copy(dst.rearrange("p (c i) t -> p c t i", i=RUN), planes.rearrange("p t (c i) -> p c t i", i=RUN))
+            nc.scalar.copy(dst.rearrange("p (c i) t -> p c t i", i=LINE), planes.rearrange("p t (c i) -> p c t i", i=LINE))
 
         z_bf = keep.tile([P, V, PACK], BF16, align_bytes=64)
         z_cd = keep.tile([P, V], U32, align_bytes=64)
@@ -250,7 +251,7 @@ def tile_picked_sagecat_max_p_kernel(
         for t in range(PACK):
             gather_centres(narrow_planes, t, WIDE_END, V)
         nc.vector.tensor_copy(
-            c_bfs[-1][:].rearrange("p (c i) t -> p c t i", i=RUN), narrow_planes.rearrange("p t (c i) -> p c t i", i=RUN)
+            c_bfs[-1][:].rearrange("p (c i) t -> p c t i", i=LINE), narrow_planes.rearrange("p t (c i) -> p c t i", i=LINE)
         )
 
         for (v0, v1), acc_o, c_bf, queue in zip(PIECES, accs, c_bfs, (nc.sync, nc.sync, nc.scalar)):

@@ -14,8 +14,9 @@ U8 = mybir.dt.uint8
 FP8X4 = mybir.dt.float8_e4m3fn_x4
 MAX = mybir.AluOpType.max
 ADD = mybir.AluOpType.add
-SUB = mybir.AluOpType.subtract
+MULT = mybir.AluOpType.mult
 RELU = mybir.ActivationFunctionType.Relu
+COPY = mybir.ActivationFunctionType.Copy
 
 P = 128
 PACK = 4
@@ -30,16 +31,7 @@ LATE = 768
 SCALAR_SHARE = 12
 FIRST_TILE_CUTS = (0, 256, 512, LATE, 896, S)
 OTHER_TILE_BANKS = [(0, BANK), (BANK, LATE, S)]
-WIDE_END = 384
-PIECES = ((0, 256), (256, WIDE_END), (WIDE_END, V))
-
-LAST_TILE_SLOTS = 0
-BASE_SLOTS = 4
-OTHER_SLOTS = 7
-CENTRE_SLOTS = 13
-W23_SLOTS = 14
-PAIR_SLOTS = 16
-SLOTS = 24
+HALF = V // 2
 
 
 def tile_picked_sagecat_max_p_kernel(
@@ -48,9 +40,8 @@ def tile_picked_sagecat_max_p_kernel(
     nc = tc.nc
     with ExitStack() as ctx:
         keep = ctx.enter_context(tc.tile_pool(name="keep", bufs=1))
-        ring = ctx.enter_context(tc.tile_pool(name="ring", bufs=2))
         psum_h = ctx.enter_context(tc.psum_pool(name="psum_h", bufs=len(FIRST_TILE_CUTS) - 1))
-        psum_o = ctx.enter_context(tc.psum_pool(name="psum_o", bufs=len(PIECES)))
+        psum_o = ctx.enter_context(tc.psum_pool(name="psum_o", bufs=2))
 
         def load_list(src, name):
             tile = keep.tile(list(src.shape), U16, name=name)
@@ -67,6 +58,7 @@ def tile_picked_sagecat_max_p_kernel(
         nc.sync.dma_start(table_words[:].bitcast(I32), x_words[0].rearrange("p c r -> p (c r)").bitcast(I32))
         w1_raw = keep.tile([P, PACK, H], F32)
         nc.sync.dma_start(w1_raw[:], w1.rearrange("(p j) c -> p j c", j=PACK))
+        cen_sb = load_list(cen, "cen_sb")
         pos_sb.append(load_list(pos2, "pos2_sb"))
         pos_sb.append(load_list(pos3, "pos3_sb"))
         pos_sb.append(load_list(pos4, "pos4_sb"))
@@ -77,7 +69,6 @@ def tile_picked_sagecat_max_p_kernel(
             for b in range(RUN):
                 nc.sync.dma_start(raw[b:P:RUN], rows[b])
             w23_raw.append(raw)
-        cen_sb = load_list(cen, "cen_sb")
 
         x_sc = keep.tile([P, S], U8, align_bytes=64)
         nc.vector.tensor_copy(x_sc[:], table_scales[:].indirect(offs_sb[:]))
@@ -137,122 +128,100 @@ def tile_picked_sagecat_max_p_kernel(
                 quantise_w1(2, 4, w1_bf23[:])
             h.append(ht)
 
-        last = PACK - 1
-        z_planes = keep.tile([P, PACK, V], BF16)
-        nb = keep.tile([P, SLOTS * V], BF16, align_bytes=64)
-
-        def slot(s, count=1):
-            return nb[:, s * V : (s + count) * V]
-
-        pairs = slot(PAIR_SLOTS, 2 * PACK).rearrange("p (e t v) -> p e t v", e=2, t=PACK)
-
-        def gather_neighbours(dst, t, d):
-            nc.vector.tensor_copy(dst, h[t][:].indirect(pos_sb[d][:]))
-
-        maxima = [(t, e) for t in range(last) for e in range(2)]
-        bases = [slot(BASE_SLOTS + u) for u in range(3)] + [slot(CENTRE_SLOTS), slot(W23_SLOTS), pairs[:, 0, last, :]]
-        others = [slot(OTHER_SLOTS + u) for u in range(len(maxima))]
-        gains = []
-
-        def add_gain(u):
-            t, e = maxima[u]
-            nc.gpsimd.tensor_tensor(pairs[:, e, t, :], bases[u], gains[u][:], ADD)
-
-        for u, (t, e) in enumerate(maxima):
-            gather_neighbours(bases[u], t, 2 * e)
-            gather_neighbours(others[u], t, 2 * e + 1)
-            diff = ring.tile([P, V], F32)
-            if u == len(maxima) - 1:
-                gain = keep.tile([P, V], F32, align_bytes=64, tag="late", name="last_gain")
+        def gather(on_vector, dst, t, offsets):
+            if on_vector:
+                nc.vector.tensor_copy(dst, h[t][:].indirect(offsets))
             else:
-                gain = ring.tile([P, V], F32)
-            nc.gpsimd.tensor_tensor(diff[:], others[u], bases[u], SUB)
-            nc.scalar.activation(gain[:], diff[:], RELU)
-            gains.append(gain)
-            if u > 0:
-                add_gain(u - 1)
-        add_gain(len(maxima) - 1)
-        for d in range(DEGREE):
-            gather_neighbours(slot(LAST_TILE_SLOTS + d), last, d)
+                nc.scalar.activation(dst, h[t][:].indirect(offsets), COPY)
 
-        wide_planes = slot(CENTRE_SLOTS, PACK).rearrange("p (t v) -> p t v", t=PACK)[:, :, :WIDE_END]
+        def halves_of(offsets):
+            columns = HALF // LIST_COLUMN
+            return [offsets[:, :columns], offsets[:, columns:]]
 
-        def gather_centres(planes, t, v0, v1):
-            nc.vector.tensor_copy(planes[:, t, :], h[t][:].indirect(cen_sb[:, v0 // LIST_COLUMN : v1 // LIST_COLUMN]))
-
-        gather_centres(wide_planes, 0, 0, WIDE_END)
-        nc.vector.tensor_tensor(
-            pairs[:, :, last, :],
-            slot(LAST_TILE_SLOTS, 2).rearrange("p (e v) -> p e v", e=2),
-            slot(LAST_TILE_SLOTS + 2, 2).rearrange("p (e v) -> p e v", e=2),
-            MAX,
-        )
-        w23_bf = slot(W23_SLOTS, 2).rearrange("p (a n j) -> p a n j", a=2, j=PACK)
+        second = keep.tile([P, 2 * N * PACK + V * PACK], BF16, align_bytes=64)
+        w23_bf = second[:, : 2 * N * PACK].rearrange("p (a n j) -> p a n j", a=2, j=PACK)
+        c_bf = second[:, 2 * N * PACK :].rearrange("p (v t) -> p v t", t=PACK)
         for a in range(2):
-            nc.scalar.copy(
-                w23_bf[:, a].rearrange("p (c i) j -> p c j i", i=RUN),
-                w23_raw[a][:].rearrange("p j (c i) -> p c j i", i=RUN),
-            )
-        w23_cd = keep.tile([P, 2 * N], U32, align_bytes=64, tag="late")
-        w23_sc = keep.tile([P, 2 * N], U8, align_bytes=64)
-        nc.vector.quantize_mx(out=w23_cd[:].bitcast(FP8X4), scales=w23_sc[:], in_=slot(W23_SLOTS, 2))
-        halves = (slice(0, V // 2), slice(V // 2, V))
-        for half in halves:
-            nc.vector.tensor_tensor(z_planes[:, :, half], pairs[:, 0, :, half], pairs[:, 1, :, half], MAX)
-        for t in range(1, PACK):
-            gather_centres(wide_planes, t, 0, WIDE_END)
+            nc.gpsimd.tensor_scalar(w23_bf[:, a], w23_raw[a][:].rearrange("p j n -> p n j"), 1.0, 0.0, MULT, ADD)
 
-        def interleave(dst, planes):
-            nc.scalar.copy(dst.rearrange("p (c i) t -> p c t i", i=LINE), planes.rearrange("p t (c i) -> p c t i", i=LINE))
+        c_planes = keep.tile([P, PACK * V], BF16, align_bytes=64)
+        for t in range(PACK):
+            gather(t == 0, c_planes[:, t * V : (t + 1) * V], t, cen_sb[:])
+        nc.gpsimd.tensor_scalar(c_bf, c_planes[:].rearrange("p (t v) -> p v t", t=PACK), 1.0, 0.0, MULT, ADD)
 
-        z_bf = keep.tile([P, V, PACK], BF16, align_bytes=64)
-        z_cd = keep.tile([P, V], U32, align_bytes=64)
-        z_sc = keep.tile([P, V], U8, align_bytes=64)
+        nb01 = keep.tile([P, 2 * DEGREE * V], BF16, align_bytes=64)
+        for t in range(2):
+            for d in range(DEGREE):
+                gather(True, nb01[:, (t * DEGREE + d) * V : (t * DEGREE + d + 1) * V], t, pos_sb[d][:])
+        nb2 = keep.tile([P, DEGREE * V], BF16, align_bytes=64)
+        for d in range(DEGREE):
+            gather(False, nb2[:, d * V : (d + 1) * V], 2, pos_sb[d][:])
+        nb3 = [keep.tile([P, DEGREE * HALF], BF16, align_bytes=64, name="nb3_%d" % e) for e in range(2)]
+        for e in range(2):
+            for d in range(DEGREE):
+                gather(False, nb3[e][:, d * HALF : (d + 1) * HALF], 3, halves_of(pos_sb[d])[e])
 
-        def open_group(v0, v1):
+        z_flat = keep.tile([P, PACK * V], BF16, align_bytes=64)
+        z_planes = z_flat[:].rearrange("p (e t v) -> p e t v", e=2, t=PACK)
+        both = nb01[:].rearrange("p (t u x) -> p t u x", t=2, u=2)
+        pairs01 = c_planes[:].rearrange("p (t x) -> p t x", t=2)
+        nc.vector.tensor_tensor(pairs01, both[:, :, 0], both[:, :, 1], MAX)
+        codes = keep.tile([P, 2 * N + V], U32, align_bytes=64)
+        scales = keep.tile([P, 2 * N + V], U8, align_bytes=64)
+        cut = 2 * N + HALF
+        nc.vector.quantize_mx(out=codes[:, :cut].bitcast(FP8X4), scales=scales[:, :cut], in_=second[:, : PACK * cut])
+        rounds = c_planes[:].rearrange("p (t u e v) -> p u e t v", t=2, u=2, e=2)
+        nc.vector.tensor_tensor(z_planes[:, :, 0:2, :], rounds[:, 0], rounds[:, 1], MAX)
+        nc.vector.quantize_mx(out=codes[:, cut:].bitcast(FP8X4), scales=scales[:, cut:], in_=second[:, PACK * cut :])
+
+        accs = []
+        for e in range(2):
             acc_o = psum_o.tile([P, BANK], F32)
+            cols = slice(2 * N + e * HALF, 2 * N + (e + 1) * HALF)
             nc.tensor.matmul_mx(
-                out=acc_o[:, : v1 - v0],
-                lhsT=w23_cd[:, :N].bitcast(FP8X4),
-                lhsT_scale=w23_sc[:, :N],
-                rhs=z_cd[:, v0:v1].bitcast(FP8X4),
-                rhs_scale=z_sc[:, v0:v1],
+                out=acc_o[:, :HALF],
+                lhsT=codes[:, N : 2 * N].bitcast(FP8X4),
+                lhsT_scale=scales[:, N : 2 * N],
+                rhs=codes[:, cols].bitcast(FP8X4),
+                rhs_scale=scales[:, cols],
                 start=True,
                 stop=False,
             )
-            return acc_o
+            accs.append(acc_o)
 
-        def close_group(v0, v1, acc_o, c_bf, queue):
-            c_cd = keep.tile([P, v1 - v0], U32, align_bytes=64, name="c_cd%d" % v0)
-            c_sc = keep.tile([P, v1 - v0], U8, align_bytes=64, name="c_sc%d" % v0)
-            nc.vector.quantize_mx(out=c_cd[:].bitcast(FP8X4), scales=c_sc[:], in_=c_bf[:].rearrange("p v t -> p (v t)"))
+        pairs2 = keep.tile([P, 2 * V], BF16, align_bytes=64)
+        nc.vector.tensor_tensor(pairs2[:], nb2[:, : 2 * V], nb2[:, 2 * V :], MAX)
+        rounds2 = pairs2[:].rearrange("p (u e v) -> p u e v", u=2, e=2)
+        nc.vector.tensor_tensor(z_planes[:, :, 2, :], rounds2[:, 0], rounds2[:, 1], MAX)
+
+        def finish(e, queue):
+            z_bf = keep.tile([P, HALF, PACK], BF16, align_bytes=64, name="z_bf%d" % e)
+            nc.vector.tensor_copy(
+                z_bf[:].rearrange("p (c i) t -> p c t i", i=LINE), z_planes[:, e].rearrange("p t (c i) -> p c t i", i=LINE)
+            )
+            z_cd = keep.tile([P, HALF], U32, align_bytes=64, name="z_cd%d" % e)
+            z_sc = keep.tile([P, HALF], U8, align_bytes=64, name="z_sc%d" % e)
+            nc.vector.quantize_mx(out=z_cd[:].bitcast(FP8X4), scales=z_sc[:], in_=z_bf[:].rearrange("p v t -> p (v t)"))
             nc.tensor.matmul_mx(
-                out=acc_o[:, : v1 - v0],
-                lhsT=w23_cd[:, N:].bitcast(FP8X4),
-                lhsT_scale=w23_sc[:, N:],
-                rhs=c_cd[:].bitcast(FP8X4),
-                rhs_scale=c_sc[:],
+                out=accs[e][:, :HALF],
+                lhsT=codes[:, :N].bitcast(FP8X4),
+                lhsT_scale=scales[:, :N],
+                rhs=z_cd[:].bitcast(FP8X4),
+                rhs_scale=z_sc[:],
                 start=False,
                 stop=True,
             )
-            res = keep.tile([P, v1 - v0], F32, name="res%d" % v0)
-            nc.scalar.copy(res[:], acc_o[:, : v1 - v0])
-            queue.dma_start(out[:, v0:v1], res[:])
+            res = keep.tile([P, HALF], F32, name="res%d" % e)
+            nc.scalar.copy(res[:], accs[e][:, :HALF])
+            queue.dma_start(out[:, e * HALF : (e + 1) * HALF], res[:])
 
-        for half in halves:
-            interleave(z_bf[:, half], z_planes[:, :, half])
-        nc.vector.quantize_mx(out=z_cd[:].bitcast(FP8X4), scales=z_sc[:], in_=z_bf[:].rearrange("p v t -> p (v t)"))
-        accs = [open_group(v0, v1) for v0, v1 in PIECES]
-        c_bfs = [keep.tile([P, v1 - v0, PACK], BF16, align_bytes=64, name="c_bf%d" % v0) for v0, v1 in PIECES]
-        for (v0, v1), c_bf in zip(PIECES[:-1], c_bfs):
-            interleave(c_bf[:], wide_planes[:, :, v0:v1])
-
-        narrow_planes = z_planes[:, :, WIDE_END:]
-        for t in range(PACK):
-            gather_centres(narrow_planes, t, WIDE_END, V)
-        nc.vector.tensor_copy(
-            c_bfs[-1][:].rearrange("p (c i) t -> p c t i", i=LINE), narrow_planes.rearrange("p t (c i) -> p c t i", i=LINE)
-        )
-
-        for (v0, v1), acc_o, c_bf, queue in zip(PIECES, accs, c_bfs, (nc.sync, nc.sync, nc.scalar)):
-            close_group(v0, v1, acc_o, c_bf, queue)
+        pairs3 = keep.tile([P, 2 * HALF], BF16, align_bytes=64)
+        nc.vector.tensor_tensor(pairs3[:], nb3[0][:, : 2 * HALF], nb3[0][:, 2 * HALF :], MAX)
+        nc.vector.tensor_tensor(z_planes[:, 0, 3, :], pairs3[:, :HALF], pairs3[:, HALF:], MAX)
+        run_a = keep.tile([P, HALF], BF16, align_bytes=64)
+        run_b = keep.tile([P, HALF], BF16, align_bytes=64)
+        nc.vector.tensor_tensor(run_a[:], nb3[1][:, :HALF], nb3[1][:, HALF : 2 * HALF], MAX)
+        finish(0, nc.sync)
+        nc.vector.tensor_tensor(run_b[:], run_a[:], nb3[1][:, 2 * HALF : 3 * HALF], MAX)
+        nc.vector.tensor_tensor(z_planes[:, 1, 3, :], run_b[:], nb3[1][:, 3 * HALF :], MAX)
+        finish(1, nc.scalar)

@@ -31,6 +31,8 @@ LATE = 768
 SCALAR_SHARE = 12
 FIRST_TILE_CUTS = (0, 256, 512, LATE, 896, S)
 OTHER_TILE_BANKS = [(0, BANK), (BANK, LATE, S)]
+QUARTER = V // 4
+PIECES = ((0, 256), (256, 384), (384, V))
 HALF = V // 2
 
 
@@ -41,7 +43,7 @@ def tile_picked_sagecat_max_p_kernel(
     with ExitStack() as ctx:
         keep = ctx.enter_context(tc.tile_pool(name="keep", bufs=1))
         psum_h = ctx.enter_context(tc.psum_pool(name="psum_h", bufs=len(FIRST_TILE_CUTS) - 1))
-        psum_o = ctx.enter_context(tc.psum_pool(name="psum_o", bufs=2))
+        psum_o = ctx.enter_context(tc.psum_pool(name="psum_o", bufs=3))
 
         def load_list(src, name):
             tile = keep.tile(list(src.shape), U16, name=name)
@@ -120,7 +122,7 @@ def tile_picked_sagecat_max_p_kernel(
                         start=True,
                         stop=True,
                     )
-                if t == 0 and cuts[0] == FIRST_TILE_CUTS[2]:
+                if (t == 0 and cuts[0] == FIRST_TILE_CUTS[2]) or (t == 1 and cuts[0] == 0):
                     nc.vector.tensor_scalar_max(ht[:, cuts[0] : cuts[-1]], acc[:, : cuts[-1] - cuts[0]], 0.0)
                 else:
                     nc.scalar.activation(ht[:, cuts[0] : cuts[-1]], acc[:, : cuts[-1] - cuts[0]], RELU)
@@ -133,10 +135,6 @@ def tile_picked_sagecat_max_p_kernel(
                 nc.vector.tensor_copy(dst, h[t][:].indirect(offsets))
             else:
                 nc.scalar.activation(dst, h[t][:].indirect(offsets), COPY)
-
-        def halves_of(offsets):
-            columns = HALF // LIST_COLUMN
-            return [offsets[:, :columns], offsets[:, columns:]]
 
         second = keep.tile([P, 2 * N * PACK + V * PACK], BF16, align_bytes=64)
         w23_bf = second[:, : 2 * N * PACK].rearrange("p (a n j) -> p a n j", a=2, j=PACK)
@@ -156,13 +154,14 @@ def tile_picked_sagecat_max_p_kernel(
         nb2 = keep.tile([P, DEGREE * V], BF16, align_bytes=64)
         for d in range(DEGREE):
             gather(False, nb2[:, d * V : (d + 1) * V], 2, pos_sb[d][:])
-        nb3 = [keep.tile([P, DEGREE * HALF], BF16, align_bytes=64, name="nb3_%d" % e) for e in range(2)]
-        for e in range(2):
+        nb3 = [keep.tile([P, DEGREE * (v1 - v0)], BF16, align_bytes=64, name="nb3_%d" % v0) for v0, v1 in PIECES]
+        for e, (v0, v1) in enumerate(PIECES):
             for d in range(DEGREE):
-                gather(False, nb3[e][:, d * HALF : (d + 1) * HALF], 3, halves_of(pos_sb[d])[e])
+                offsets = pos_sb[d][:, v0 // LIST_COLUMN : v1 // LIST_COLUMN]
+                gather(False, nb3[e][:, d * (v1 - v0) : (d + 1) * (v1 - v0)], 3, offsets)
 
         z_flat = keep.tile([P, PACK * V], BF16, align_bytes=64)
-        z_planes = z_flat[:].rearrange("p (e t v) -> p e t v", e=2, t=PACK)
+        z_planes = z_flat[:].rearrange("p (q t v) -> p q t v", q=4, t=PACK)
         both = nb01[:].rearrange("p (t u x) -> p t u x", t=2, u=2)
         pairs01 = c_planes[:].rearrange("p (t x) -> p t x", t=2)
         nc.vector.tensor_tensor(pairs01, both[:, :, 0], both[:, :, 1], MAX)
@@ -170,16 +169,16 @@ def tile_picked_sagecat_max_p_kernel(
         scales = keep.tile([P, 2 * N + V], U8, align_bytes=64)
         cut = 2 * N + HALF
         nc.vector.quantize_mx(out=codes[:, :cut].bitcast(FP8X4), scales=scales[:, :cut], in_=second[:, : PACK * cut])
-        rounds = c_planes[:].rearrange("p (t u e v) -> p u e t v", t=2, u=2, e=2)
+        rounds = c_planes[:].rearrange("p (t u q v) -> p u q t v", t=2, u=2, q=4)
         nc.vector.tensor_tensor(z_planes[:, :, 0:2, :], rounds[:, 0], rounds[:, 1], MAX)
         nc.vector.quantize_mx(out=codes[:, cut:].bitcast(FP8X4), scales=scales[:, cut:], in_=second[:, PACK * cut :])
 
         accs = []
-        for e in range(2):
+        for v0, v1 in PIECES:
             acc_o = psum_o.tile([P, BANK], F32)
-            cols = slice(2 * N + e * HALF, 2 * N + (e + 1) * HALF)
+            cols = slice(2 * N + v0, 2 * N + v1)
             nc.tensor.matmul_mx(
-                out=acc_o[:, :HALF],
+                out=acc_o[:, : v1 - v0],
                 lhsT=codes[:, N : 2 * N].bitcast(FP8X4),
                 lhsT_scale=scales[:, N : 2 * N],
                 rhs=codes[:, cols].bitcast(FP8X4),
@@ -189,21 +188,37 @@ def tile_picked_sagecat_max_p_kernel(
             )
             accs.append(acc_o)
 
-        pairs2 = keep.tile([P, 2 * V], BF16, align_bytes=64)
-        nc.vector.tensor_tensor(pairs2[:], nb2[:, : 2 * V], nb2[:, 2 * V :], MAX)
-        rounds2 = pairs2[:].rearrange("p (u e v) -> p u e v", u=2, e=2)
+        pairs2 = nb01[:, : 2 * V]
+        nc.vector.tensor_tensor(pairs2, nb2[:, : 2 * V], nb2[:, 2 * V :], MAX)
+        rounds2 = pairs2.rearrange("p (u q v) -> p u q v", u=2, q=4)
         nc.vector.tensor_tensor(z_planes[:, :, 2, :], rounds2[:, 0], rounds2[:, 1], MAX)
 
-        def finish(e, queue):
-            z_bf = keep.tile([P, HALF, PACK], BF16, align_bytes=64, name="z_bf%d" % e)
-            nc.vector.tensor_copy(
-                z_bf[:].rearrange("p (c i) t -> p c t i", i=LINE), z_planes[:, e].rearrange("p t (c i) -> p c t i", i=LINE)
+        z_bfs = [keep.tile([P, (v1 - v0) * PACK], BF16, align_bytes=64, name="z_bf%d" % v0) for v0, v1 in PIECES]
+        pairs3 = [nb01[:, 2 * (V + v0) : 2 * (V + v1)] for v0, v1 in PIECES]
+
+        def first_round(e):
+            width = PIECES[e][1] - PIECES[e][0]
+            nc.vector.tensor_tensor(pairs3[e], nb3[e][:, : 2 * width], nb3[e][:, 2 * width :], MAX)
+
+        def second_round(e):
+            v0, v1 = PIECES[e]
+            both = pairs3[e].rearrange("p (u q v) -> p u q v", u=2, v=QUARTER)
+            nc.vector.tensor_tensor(z_planes[:, v0 // QUARTER : v1 // QUARTER, 3, :], both[:, 0], both[:, 1], MAX)
+
+        def interleave(e, q, copy):
+            at = (q * QUARTER - PIECES[e][0]) * PACK
+            copy(
+                z_bfs[e][:, at : at + QUARTER * PACK].rearrange("p (c i t) -> p c t i", i=LINE, t=PACK),
+                z_planes[:, q].rearrange("p t (c i) -> p c t i", i=LINE),
             )
-            z_cd = keep.tile([P, HALF], U32, align_bytes=64, name="z_cd%d" % e)
-            z_sc = keep.tile([P, HALF], U8, align_bytes=64, name="z_sc%d" % e)
-            nc.vector.quantize_mx(out=z_cd[:].bitcast(FP8X4), scales=z_sc[:], in_=z_bf[:].rearrange("p v t -> p (v t)"))
+
+        def finish(e, queue):
+            v0, v1 = PIECES[e]
+            z_cd = keep.tile([P, v1 - v0], U32, align_bytes=64, name="z_cd%d" % e)
+            z_sc = keep.tile([P, v1 - v0], U8, align_bytes=64, name="z_sc%d" % e)
+            nc.vector.quantize_mx(out=z_cd[:].bitcast(FP8X4), scales=z_sc[:], in_=z_bfs[e][:])
             nc.tensor.matmul_mx(
-                out=accs[e][:, :HALF],
+                out=accs[e][:, : v1 - v0],
                 lhsT=codes[:, :N].bitcast(FP8X4),
                 lhsT_scale=scales[:, :N],
                 rhs=z_cd[:].bitcast(FP8X4),
@@ -211,17 +226,22 @@ def tile_picked_sagecat_max_p_kernel(
                 start=False,
                 stop=True,
             )
-            res = keep.tile([P, HALF], F32, name="res%d" % e)
-            nc.scalar.copy(res[:], accs[e][:, :HALF])
-            queue.dma_start(out[:, e * HALF : (e + 1) * HALF], res[:])
+            res = keep.tile([P, v1 - v0], F32, name="res%d" % e)
+            nc.scalar.copy(res[:], accs[e][:, : v1 - v0])
+            queue.dma_start(out[:, v0:v1], res[:])
 
-        pairs3 = keep.tile([P, 2 * HALF], BF16, align_bytes=64)
-        nc.vector.tensor_tensor(pairs3[:], nb3[0][:, : 2 * HALF], nb3[0][:, 2 * HALF :], MAX)
-        nc.vector.tensor_tensor(z_planes[:, 0, 3, :], pairs3[:, :HALF], pairs3[:, HALF:], MAX)
-        run_a = keep.tile([P, HALF], BF16, align_bytes=64)
-        run_b = keep.tile([P, HALF], BF16, align_bytes=64)
-        nc.vector.tensor_tensor(run_a[:], nb3[1][:, :HALF], nb3[1][:, HALF : 2 * HALF], MAX)
+        first_round(0)
+        second_round(0)
+        interleave(0, 0, nc.vector.tensor_copy)
+        first_round(1)
+        interleave(0, 1, nc.vector.tensor_copy)
+        second_round(1)
+        interleave(1, 2, nc.scalar.copy)
+        last = nb3[2]
+        nc.vector.tensor_tensor(pairs3[2][:, :QUARTER], last[:, :QUARTER], last[:, QUARTER : 2 * QUARTER], MAX)
         finish(0, nc.sync)
-        nc.vector.tensor_tensor(run_b[:], run_a[:], nb3[1][:, 2 * HALF : 3 * HALF], MAX)
-        nc.vector.tensor_tensor(z_planes[:, 1, 3, :], run_b[:], nb3[1][:, 3 * HALF :], MAX)
-        finish(1, nc.scalar)
+        nc.vector.tensor_tensor(pairs3[2][:, QUARTER:], pairs3[2][:, :QUARTER], last[:, 2 * QUARTER : 3 * QUARTER], MAX)
+        nc.vector.tensor_tensor(z_planes[:, 3, 3, :], pairs3[2][:, QUARTER:], last[:, 3 * QUARTER :], MAX)
+        interleave(2, 3, nc.vector.tensor_copy)
+        finish(1, nc.sync)
+        finish(2, nc.scalar)

@@ -56,7 +56,7 @@ def tile_picked_sagecat_max_p_kernel(
         pos_sb = [load_list(pos1, "pos1_sb")]
         for r in range(SCALE_ROWS):
             nc.sync.dma_start(table_scales[r:P:QUADRANT, :].bitcast(I32), x_scales[0, r::SCALE_ROWS, :].bitcast(I32))
-        table_words = keep.tile([P, T], U32, align_bytes=64)
+        table_words = keep.tile([P, T], U32, align_bytes=64, tag="words")
         nc.sync.dma_start(table_words[:].bitcast(I32), x_words[0].rearrange("p c r -> p (c r)").bitcast(I32))
         w1_raw = keep.tile([P, PACK, H], F32)
         nc.sync.dma_start(w1_raw[:], w1.rearrange("(p j) c -> p j c", j=PACK))
@@ -94,17 +94,19 @@ def tile_picked_sagecat_max_p_kernel(
 
         w1_bf0 = keep.tile([P, 1, P, PACK], BF16, align_bytes=64, tag="first")
         w1_bf1 = keep.tile([P, 1, P, PACK], BF16, align_bytes=64)
-        w1_bf23 = keep.tile([P, 2, P, PACK], BF16, align_bytes=64)
+        w1_bf2 = keep.tile([P, 1, P, PACK], BF16, align_bytes=64)
         nc.scalar.copy(cast_view(w1_bf0)[:, 0, :SCALAR_SHARE], dealt[:, 0, :SCALAR_SHARE])
         nc.vector.tensor_copy(cast_view(w1_bf0)[:, 0, SCALAR_SHARE:], dealt[:, 0, SCALAR_SHARE:])
-        nc.vector.tensor_copy(cast_view(w1_bf23)[:, 1, :16], dealt[:, 3, :16])
         quantise_w1(0, 1, w1_bf0[:])
         x_late = keep.tile([P, S - LATE], U32, align_bytes=64, tag="first")
         nc.vector.tensor_copy(x_late[:], table_words[:].indirect(offs_sb[:, LATE // LIST_COLUMN :]))
         nc.scalar.copy(cast_view(w1_bf1)[:, 0], dealt[:, 1])
-        nc.scalar.copy(cast_view(w1_bf23)[:, 0], dealt[:, 2])
-        nc.scalar.copy(cast_view(w1_bf23)[:, 1, 16:], dealt[:, 3, 16:])
+        nc.scalar.copy(cast_view(w1_bf2)[:, 0], dealt[:, 2])
         quantise_w1(1, 2, w1_bf1[:])
+        w1_bf3 = keep.tile([P, 1, P, PACK], BF16, align_bytes=64, tag="words")
+        nc.vector.tensor_copy(cast_view(w1_bf3)[:, 0], dealt[:, 3])
+        quantise_w1(2, 3, w1_bf2[:])
+        quantise_w1(3, 4, w1_bf3[:])
 
         h = []
         for t in range(PACK):
@@ -122,12 +124,7 @@ def tile_picked_sagecat_max_p_kernel(
                         start=True,
                         stop=True,
                     )
-                if (t == 0 and cuts[0] == FIRST_TILE_CUTS[2]) or (t == 1 and cuts[0] == 0):
-                    nc.vector.tensor_scalar_max(ht[:, cuts[0] : cuts[-1]], acc[:, : cuts[-1] - cuts[0]], 0.0)
-                else:
-                    nc.scalar.activation(ht[:, cuts[0] : cuts[-1]], acc[:, : cuts[-1] - cuts[0]], RELU)
-            if t == 0:
-                quantise_w1(2, 4, w1_bf23[:])
+                nc.scalar.activation(ht[:, cuts[0] : cuts[-1]], acc[:, : cuts[-1] - cuts[0]], RELU)
             h.append(ht)
 
         def gather(on_vector, dst, t, offsets):
@@ -136,7 +133,7 @@ def tile_picked_sagecat_max_p_kernel(
             else:
                 nc.scalar.activation(dst, h[t][:].indirect(offsets), COPY)
 
-        second = keep.tile([P, 2 * N * PACK + V * PACK], BF16, align_bytes=64)
+        second = keep.tile([P, 2 * N * PACK + V * PACK], BF16, align_bytes=64, tag="words")
         w23_bf = second[:, : 2 * N * PACK].rearrange("p (a n j) -> p a n j", a=2, j=PACK)
         c_bf = second[:, 2 * N * PACK :].rearrange("p (v t) -> p v t", t=PACK)
         for a in range(2):
@@ -152,13 +149,13 @@ def tile_picked_sagecat_max_p_kernel(
             for d in range(DEGREE):
                 gather(True, nb01[:, (t * DEGREE + d) * V : (t * DEGREE + d + 1) * V], t, pos_sb[d][:])
         nb2 = keep.tile([P, DEGREE * V], BF16, align_bytes=64)
-        for d in range(DEGREE):
+        gather(True, nb2[:, :HALF], 2, pos_sb[0][:, : HALF // LIST_COLUMN])
+        gather(False, nb2[:, HALF:V], 2, pos_sb[0][:, HALF // LIST_COLUMN :])
+        for d in range(1, DEGREE):
             gather(False, nb2[:, d * V : (d + 1) * V], 2, pos_sb[d][:])
-        nb3 = [keep.tile([P, DEGREE * (v1 - v0)], BF16, align_bytes=64, name="nb3_%d" % v0) for v0, v1 in PIECES]
-        for e, (v0, v1) in enumerate(PIECES):
-            for d in range(DEGREE):
-                offsets = pos_sb[d][:, v0 // LIST_COLUMN : v1 // LIST_COLUMN]
-                gather(False, nb3[e][:, d * (v1 - v0) : (d + 1) * (v1 - v0)], 3, offsets)
+        nb3 = keep.tile([P, DEGREE * V], BF16, align_bytes=64)
+        for d, v0, v1 in ((0, 0, V), (1, 0, V), (2, 0, HALF), (3, 0, HALF), (2, HALF, V), (3, HALF, 384), (3, 384, V)):
+            gather(False, nb3[:, d * V + v0 : d * V + v1], 3, pos_sb[d][:, v0 // LIST_COLUMN : v1 // LIST_COLUMN])
 
         z_flat = keep.tile([P, PACK * V], BF16, align_bytes=64)
         z_planes = z_flat[:].rearrange("p (q t v) -> p q t v", q=4, t=PACK)
@@ -190,20 +187,25 @@ def tile_picked_sagecat_max_p_kernel(
 
         pairs2 = nb01[:, : 2 * V]
         nc.vector.tensor_tensor(pairs2, nb2[:, : 2 * V], nb2[:, 2 * V :], MAX)
+        nc.vector.tensor_tensor(nb01[:, 2 * V : 3 * V], nb3[:, :V], nb3[:, V : 2 * V], MAX)
         rounds2 = pairs2.rearrange("p (u q v) -> p u q v", u=2, q=4)
         nc.vector.tensor_tensor(z_planes[:, :, 2, :], rounds2[:, 0], rounds2[:, 1], MAX)
 
         z_bfs = [keep.tile([P, (v1 - v0) * PACK], BF16, align_bytes=64, name="z_bf%d" % v0) for v0, v1 in PIECES]
-        pairs3 = [nb01[:, 2 * (V + v0) : 2 * (V + v1)] for v0, v1 in PIECES]
+        of_two = nb01[:, 2 * V : 3 * V]
+        of_three = nb01[:, 3 * V : 4 * V]
 
-        def first_round(e):
-            width = PIECES[e][1] - PIECES[e][0]
-            nc.vector.tensor_tensor(pairs3[e], nb3[e][:, : 2 * width], nb3[e][:, 2 * width :], MAX)
+        def third(v0, v1):
+            nc.vector.tensor_tensor(of_three[:, v0:v1], of_two[:, v0:v1], nb3[:, 2 * V + v0 : 2 * V + v1], MAX)
 
-        def second_round(e):
+        def fourth(e):
             v0, v1 = PIECES[e]
-            both = pairs3[e].rearrange("p (u q v) -> p u q v", u=2, v=QUARTER)
-            nc.vector.tensor_tensor(z_planes[:, v0 // QUARTER : v1 // QUARTER, 3, :], both[:, 0], both[:, 1], MAX)
+            nc.vector.tensor_tensor(
+                z_planes[:, v0 // QUARTER : v1 // QUARTER, 3, :],
+                of_three[:, v0:v1].rearrange("p (q v) -> p q v", v=QUARTER),
+                nb3[:, 3 * V + v0 : 3 * V + v1].rearrange("p (q v) -> p q v", v=QUARTER),
+                MAX,
+            )
 
         def interleave(e, q, copy):
             at = (q * QUARTER - PIECES[e][0]) * PACK
@@ -212,7 +214,7 @@ def tile_picked_sagecat_max_p_kernel(
                 z_planes[:, q].rearrange("p t (c i) -> p c t i", i=LINE),
             )
 
-        def finish(e, queue):
+        def finish(e, copy, queue):
             v0, v1 = PIECES[e]
             z_cd = keep.tile([P, v1 - v0], U32, align_bytes=64, name="z_cd%d" % e)
             z_sc = keep.tile([P, v1 - v0], U8, align_bytes=64, name="z_sc%d" % e)
@@ -227,21 +229,18 @@ def tile_picked_sagecat_max_p_kernel(
                 stop=True,
             )
             res = keep.tile([P, v1 - v0], F32, name="res%d" % e)
-            nc.scalar.copy(res[:], accs[e][:, : v1 - v0])
+            copy(res[:], accs[e][:, : v1 - v0])
             queue.dma_start(out[:, v0:v1], res[:])
 
-        first_round(0)
-        second_round(0)
+        third(0, HALF)
+        fourth(0)
+        third(HALF, V)
         interleave(0, 0, nc.vector.tensor_copy)
-        first_round(1)
         interleave(0, 1, nc.vector.tensor_copy)
-        second_round(1)
+        fourth(1)
         interleave(1, 2, nc.scalar.copy)
-        last = nb3[2]
-        nc.vector.tensor_tensor(pairs3[2][:, :QUARTER], last[:, :QUARTER], last[:, QUARTER : 2 * QUARTER], MAX)
-        finish(0, nc.sync)
-        nc.vector.tensor_tensor(pairs3[2][:, QUARTER:], pairs3[2][:, :QUARTER], last[:, 2 * QUARTER : 3 * QUARTER], MAX)
-        nc.vector.tensor_tensor(z_planes[:, 3, 3, :], pairs3[2][:, QUARTER:], last[:, 3 * QUARTER :], MAX)
+        finish(0, nc.scalar.copy, nc.sync)
+        fourth(2)
         interleave(2, 3, nc.vector.tensor_copy)
-        finish(1, nc.sync)
-        finish(2, nc.scalar)
+        finish(1, nc.vector.tensor_copy, nc.sync)
+        finish(2, nc.scalar.copy, nc.scalar)

@@ -26,12 +26,10 @@ LIST_COLUMN = 16
 QUADRANT = 32
 SCALE_ROWS = 4
 RUN = 4
-LINE = 8
 LATE = 768
 SCALAR_SHARE = 12
 FIRST_TILE_CUTS = (0, 256, 512, LATE, 896, S)
 OTHER_TILE_BANKS = [(0, BANK), (BANK, LATE, S)]
-QUARTER = V // 4
 PIECES = ((0, 256), (256, 384), (384, V))
 HALF = V // 2
 
@@ -139,35 +137,41 @@ def tile_picked_sagecat_max_p_kernel(
         for a in range(2):
             nc.gpsimd.tensor_scalar(w23_bf[:, a], w23_raw[a][:].rearrange("p j n -> p n j"), 1.0, 0.0, MULT, ADD)
 
-        c_planes = keep.tile([P, PACK * V], BF16, align_bytes=64)
+        work = keep.tile([P, 3 * PACK * V], BF16, align_bytes=64)
+        c_planes = work[:, : PACK * V]
+        nb01 = work[:, PACK * V :]
+        rounds = work[:, : 2 * PACK * V].rearrange("p (t u v) -> p t u v", t=PACK, u=2)
         for t in range(PACK):
             gather(t == 0, c_planes[:, t * V : (t + 1) * V], t, cen_sb[:])
-        nc.gpsimd.tensor_scalar(c_bf, c_planes[:].rearrange("p (t v) -> p v t", t=PACK), 1.0, 0.0, MULT, ADD)
+        nc.gpsimd.tensor_scalar(c_bf, c_planes.rearrange("p (t v) -> p v t", t=PACK), 1.0, 0.0, MULT, ADD)
 
-        nb01 = keep.tile([P, 2 * DEGREE * V], BF16, align_bytes=64)
         for t in range(2):
             for d in range(DEGREE):
                 gather(True, nb01[:, (t * DEGREE + d) * V : (t * DEGREE + d + 1) * V], t, pos_sb[d][:])
         nb2 = keep.tile([P, DEGREE * V], BF16, align_bytes=64)
-        gather(True, nb2[:, :HALF], 2, pos_sb[0][:, : HALF // LIST_COLUMN])
-        gather(False, nb2[:, HALF:V], 2, pos_sb[0][:, HALF // LIST_COLUMN :])
-        for d in range(1, DEGREE):
-            gather(False, nb2[:, d * V : (d + 1) * V], 2, pos_sb[d][:])
+        for d in range(DEGREE):
+            gather(d == 0, nb2[:, d * V : (d + 1) * V], 2, pos_sb[d][:])
         nb3 = keep.tile([P, DEGREE * V], BF16, align_bytes=64)
-        for d, v0, v1 in ((0, 0, V), (1, 0, V), (2, 0, HALF), (3, 0, HALF), (2, HALF, V), (3, HALF, 384), (3, 384, V)):
-            gather(False, nb3[:, d * V + v0 : d * V + v1], 3, pos_sb[d][:, v0 // LIST_COLUMN : v1 // LIST_COLUMN])
 
-        z_flat = keep.tile([P, PACK * V], BF16, align_bytes=64)
-        z_planes = z_flat[:].rearrange("p (q t v) -> p q t v", q=4, t=PACK)
-        both = nb01[:].rearrange("p (t u x) -> p t u x", t=2, u=2)
-        pairs01 = c_planes[:].rearrange("p (t x) -> p t x", t=2)
-        nc.vector.tensor_tensor(pairs01, both[:, :, 0], both[:, :, 1], MAX)
+        def entries(d, v0, v1):
+            return pos_sb[d][:, v0 // LIST_COLUMN : v1 // LIST_COLUMN]
+
+        for d in range(DEGREE):
+            gather(False, nb3[:, d * V : d * V + HALF], 3, entries(d, 0, HALF))
+        for d in range(DEGREE - 1):
+            gather(False, nb3[:, d * V + HALF : (d + 1) * V], 3, entries(d, HALF, V))
+
+        both = nb01.rearrange("p (t u x) -> p t u x", t=2, u=2)
+        nc.vector.tensor_tensor(c_planes.rearrange("p (t x) -> p t x", t=2), both[:, :, 0], both[:, :, 1], MAX)
+        for v0, v1 in PIECES[1:]:
+            gather(False, rounds[:, 3, 1, v0:v1], 3, entries(3, v0, v1))
         codes = keep.tile([P, 2 * N + V], U32, align_bytes=64)
         scales = keep.tile([P, 2 * N + V], U8, align_bytes=64)
         cut = 2 * N + HALF
         nc.vector.quantize_mx(out=codes[:, :cut].bitcast(FP8X4), scales=scales[:, :cut], in_=second[:, : PACK * cut])
-        rounds = c_planes[:].rearrange("p (t u q v) -> p u q t v", t=2, u=2, q=4)
-        nc.vector.tensor_tensor(z_planes[:, :, 0:2, :], rounds[:, 0], rounds[:, 1], MAX)
+        nc.vector.tensor_tensor(work[:, PACK * V : PACK * V + 2 * V], nb2[:, : 2 * V], nb2[:, 2 * V :], MAX)
+        pairs3 = nb3[:].rearrange("p (w u v) -> p w u v", w=2, u=2)
+        nc.vector.tensor_tensor(rounds[:, 3, :, :HALF], pairs3[:, 0, :, :HALF], pairs3[:, 1, :, :HALF], MAX)
         nc.vector.quantize_mx(out=codes[:, cut:].bitcast(FP8X4), scales=scales[:, cut:], in_=second[:, PACK * cut :])
 
         accs = []
@@ -185,33 +189,15 @@ def tile_picked_sagecat_max_p_kernel(
             )
             accs.append(acc_o)
 
-        pairs2 = nb01[:, : 2 * V]
-        nc.vector.tensor_tensor(pairs2, nb2[:, : 2 * V], nb2[:, 2 * V :], MAX)
-        nc.vector.tensor_tensor(nb01[:, 2 * V : 3 * V], nb3[:, :V], nb3[:, V : 2 * V], MAX)
-        rounds2 = pairs2.rearrange("p (u q v) -> p u q v", u=2, q=4)
-        nc.vector.tensor_tensor(z_planes[:, :, 2, :], rounds2[:, 0], rounds2[:, 1], MAX)
-
         z_bfs = [keep.tile([P, (v1 - v0) * PACK], BF16, align_bytes=64, name="z_bf%d" % v0) for v0, v1 in PIECES]
-        of_two = nb01[:, 2 * V : 3 * V]
-        of_three = nb01[:, 3 * V : 4 * V]
 
-        def third(v0, v1):
-            nc.vector.tensor_tensor(of_three[:, v0:v1], of_two[:, v0:v1], nb3[:, 2 * V + v0 : 2 * V + v1], MAX)
-
-        def fourth(e):
+        def last_round(e):
             v0, v1 = PIECES[e]
             nc.vector.tensor_tensor(
-                z_planes[:, v0 // QUARTER : v1 // QUARTER, 3, :],
-                of_three[:, v0:v1].rearrange("p (q v) -> p q v", v=QUARTER),
-                nb3[:, 3 * V + v0 : 3 * V + v1].rearrange("p (q v) -> p q v", v=QUARTER),
+                z_bfs[e][:].rearrange("p (c i t) -> p c t i", i=RUN, t=PACK),
+                rounds[:, :, 0, v0:v1].rearrange("p t (c i) -> p c t i", i=RUN),
+                rounds[:, :, 1, v0:v1].rearrange("p t (c i) -> p c t i", i=RUN),
                 MAX,
-            )
-
-        def interleave(e, q, copy):
-            at = (q * QUARTER - PIECES[e][0]) * PACK
-            copy(
-                z_bfs[e][:, at : at + QUARTER * PACK].rearrange("p (c i t) -> p c t i", i=LINE, t=PACK),
-                z_planes[:, q].rearrange("p t (c i) -> p c t i", i=LINE),
             )
 
         def finish(e, copy, queue):
@@ -232,15 +218,12 @@ def tile_picked_sagecat_max_p_kernel(
             copy(res[:], accs[e][:, : v1 - v0])
             queue.dma_start(out[:, v0:v1], res[:])
 
-        third(0, HALF)
-        fourth(0)
-        third(HALF, V)
-        interleave(0, 0, nc.vector.tensor_copy)
-        interleave(0, 1, nc.vector.tensor_copy)
-        fourth(1)
-        interleave(1, 2, nc.scalar.copy)
+        last_round(0)
+        of_two = nb2[:, :HALF]
+        nc.vector.tensor_tensor(of_two, nb3[:, HALF:V], nb3[:, V + HALF : 2 * V], MAX)
         finish(0, nc.scalar.copy, nc.sync)
-        fourth(2)
-        interleave(2, 3, nc.vector.tensor_copy)
-        finish(1, nc.vector.tensor_copy, nc.sync)
-        finish(2, nc.scalar.copy, nc.scalar)
+        nc.vector.tensor_tensor(rounds[:, 3, 0, HALF:], of_two, nb3[:, 2 * V + HALF : 3 * V], MAX)
+        last_round(1)
+        last_round(2)
+        finish(1, nc.scalar.copy, nc.sync)
+        finish(2, nc.vector.tensor_copy, nc.scalar)

@@ -31,6 +31,7 @@ SCALAR_SHARE = 12
 FIRST_TILE_CUTS = (0, 256, 512, LATE, 896, S)
 OTHER_TILE_BANKS = [(0, BANK), (BANK, LATE, S)]
 PIECES = ((0, 256), (256, 384), (384, V))
+SHARED = 384
 HALF = V // 2
 
 
@@ -149,8 +150,10 @@ def tile_picked_sagecat_max_p_kernel(
             for d in range(DEGREE):
                 gather(True, nb01[:, (t * DEGREE + d) * V : (t * DEGREE + d + 1) * V], t, pos_sb[d][:])
         nb2 = keep.tile([P, DEGREE * V], BF16, align_bytes=64)
-        for d in range(DEGREE):
-            gather(d == 0, nb2[:, d * V : (d + 1) * V], 2, pos_sb[d][:])
+        gather(True, nb2[:, :SHARED], 2, pos_sb[0][:, : SHARED // LIST_COLUMN])
+        gather(False, nb2[:, SHARED:V], 2, pos_sb[0][:, SHARED // LIST_COLUMN :])
+        for d in range(1, DEGREE):
+            gather(False, nb2[:, d * V : (d + 1) * V], 2, pos_sb[d][:])
         nb3 = keep.tile([P, DEGREE * V], BF16, align_bytes=64)
 
         def entries(d, v0, v1):
@@ -225,5 +228,5 @@ def tile_picked_sagecat_max_p_kernel(
         nc.vector.tensor_tensor(rounds[:, 3, 0, HALF:], of_two, nb3[:, 2 * V + HALF : 3 * V], MAX)
         last_round(1)
         last_round(2)
-        finish(1, nc.scalar.copy, nc.sync)
+        finish(1, nc.scalar.copy, nc.scalar)
         finish(2, nc.vector.tensor_copy, nc.scalar)

@@ -31,7 +31,7 @@ SCALAR_SHARE = 12
 FIRST_TILE_CUTS = (0, 256, 512, LATE, 896, S)
 OTHER_TILE_BANKS = [(0, BANK), (BANK, LATE, S)]
 PIECES = ((0, 256), (256, 384), (384, V))
-SHARED = 384
+SHARED = 256
 HALF = V // 2
 
 
@@ -111,6 +111,8 @@ def tile_picked_sagecat_max_p_kernel(
         for t in range(PACK):
             ht = keep.tile([P, S], F32, name="h%d" % t)
             banks = [(s0, s1) for s0, s1 in zip(FIRST_TILE_CUTS, FIRST_TILE_CUTS[1:])] if t == 0 else OTHER_TILE_BANKS
+            if t == 1:
+                banks = [(0, 256), (256, BANK, LATE), (LATE, S)]
             for cuts in banks:
                 acc = psum_h.tile([P, BANK], F32)
                 for s0, s1 in zip(cuts, cuts[1:]):
@@ -123,7 +125,10 @@ def tile_picked_sagecat_max_p_kernel(
                         start=True,
                         stop=True,
                     )
-                nc.scalar.activation(ht[:, cuts[0] : cuts[-1]], acc[:, : cuts[-1] - cuts[0]], RELU)
+                if t == 1 and cuts[0] == 0:
+                    nc.vector.tensor_scalar_max(ht[:, cuts[0] : cuts[-1]], acc[:, : cuts[-1] - cuts[0]], 0.0)
+                else:
+                    nc.scalar.activation(ht[:, cuts[0] : cuts[-1]], acc[:, : cuts[-1] - cuts[0]], RELU)
             h.append(ht)
 
         def gather(on_vector, dst, t, offsets):
@@ -149,20 +154,22 @@ def tile_picked_sagecat_max_p_kernel(
         for t in range(2):
             for d in range(DEGREE):
                 gather(True, nb01[:, (t * DEGREE + d) * V : (t * DEGREE + d + 1) * V], t, pos_sb[d][:])
-        nb2 = keep.tile([P, DEGREE * V], BF16, align_bytes=64)
-        gather(True, nb2[:, :SHARED], 2, pos_sb[0][:, : SHARED // LIST_COLUMN])
-        gather(False, nb2[:, SHARED:V], 2, pos_sb[0][:, SHARED // LIST_COLUMN :])
-        for d in range(1, DEGREE):
-            gather(False, nb2[:, d * V : (d + 1) * V], 2, pos_sb[d][:])
-        nb3 = keep.tile([P, DEGREE * V], BF16, align_bytes=64)
+        nb23 = keep.tile([P, 2 * DEGREE * V], BF16, align_bytes=64)
+        nb2 = nb23[:, : DEGREE * V]
+        nb3 = nb23[:, DEGREE * V :]
 
         def entries(d, v0, v1):
             return pos_sb[d][:, v0 // LIST_COLUMN : v1 // LIST_COLUMN]
 
+        gather(True, nb2[:, :SHARED], 2, entries(0, 0, SHARED))
+        for d in range(1, DEGREE):
+            gather(False, nb2[:, d * V : (d + 1) * V], 2, pos_sb[d][:])
         for d in range(DEGREE):
             gather(False, nb3[:, d * V : d * V + HALF], 3, entries(d, 0, HALF))
-        for d in range(DEGREE - 1):
+        for d in range(2):
             gather(False, nb3[:, d * V + HALF : (d + 1) * V], 3, entries(d, HALF, V))
+        gather(False, nb2[:, SHARED:V], 2, entries(0, SHARED, V))
+        gather(False, nb3[:, 2 * V + HALF : 3 * V], 3, entries(2, HALF, V))
 
         both = nb01.rearrange("p (t u x) -> p t u x", t=2, u=2)
         nc.vector.tensor_tensor(c_planes.rearrange("p (t x) -> p t x", t=2), both[:, :, 0], both[:, :, 1], MAX)
@@ -172,9 +179,9 @@ def tile_picked_sagecat_max_p_kernel(
         scales = keep.tile([P, 2 * N + V], U8, align_bytes=64)
         cut = 2 * N + HALF
         nc.vector.quantize_mx(out=codes[:, :cut].bitcast(FP8X4), scales=scales[:, :cut], in_=second[:, : PACK * cut])
-        nc.vector.tensor_tensor(work[:, PACK * V : PACK * V + 2 * V], nb2[:, : 2 * V], nb2[:, 2 * V :], MAX)
-        pairs3 = nb3[:].rearrange("p (w u v) -> p w u v", w=2, u=2)
-        nc.vector.tensor_tensor(rounds[:, 3, :, :HALF], pairs3[:, 0, :, :HALF], pairs3[:, 1, :, :HALF], MAX)
+        pairs = nb23[:].rearrange("p (t w u v) -> p w t u v", t=2, w=2, u=2)
+        for t in range(2):
+            nc.vector.tensor_tensor(rounds[:, 2 + t, :, :HALF], pairs[:, 0, t, :, :HALF], pairs[:, 1, t, :, :HALF], MAX)
         nc.vector.quantize_mx(out=codes[:, cut:].bitcast(FP8X4), scales=scales[:, cut:], in_=second[:, PACK * cut :])
 
         accs = []
@@ -224,8 +231,9 @@ def tile_picked_sagecat_max_p_kernel(
         last_round(0)
         of_two = nb2[:, :HALF]
         nc.vector.tensor_tensor(of_two, nb3[:, HALF:V], nb3[:, V + HALF : 2 * V], MAX)
-        finish(0, nc.scalar.copy, nc.sync)
+        nc.vector.tensor_tensor(rounds[:, 2, :, HALF:], pairs[:, 0, 0, :, HALF:], pairs[:, 1, 0, :, HALF:], MAX)
         nc.vector.tensor_tensor(rounds[:, 3, 0, HALF:], of_two, nb3[:, 2 * V + HALF : 3 * V], MAX)
+        finish(0, nc.scalar.copy, nc.sync)
         last_round(1)
         last_round(2)
         finish(1, nc.scalar.copy, nc.scalar)

@@ -28,7 +28,6 @@ SCALE_ROWS = 4
 RUN = 4
 LATE = 768
 SCALAR_SHARE = 12
-FIRST_TILE_CUTS = (0, 256, 512, LATE, 896, S)
 OTHER_TILE_BANKS = [(0, BANK), (BANK, LATE, S)]
 PIECES = ((0, 256), (256, 384), (384, V))
 SHARED = 256
@@ -41,7 +40,7 @@ def tile_picked_sagecat_max_p_kernel(
     nc = tc.nc
     with ExitStack() as ctx:
         keep = ctx.enter_context(tc.tile_pool(name="keep", bufs=1))
-        psum_h = ctx.enter_context(tc.psum_pool(name="psum_h", bufs=len(FIRST_TILE_CUTS) - 1))
+        psum_h = ctx.enter_context(tc.psum_pool(name="psum_h", bufs=5))
         psum_o = ctx.enter_context(tc.psum_pool(name="psum_o", bufs=3))
 
         def load_list(src, name):
@@ -110,9 +109,7 @@ def tile_picked_sagecat_max_p_kernel(
         h = []
         for t in range(PACK):
             ht = keep.tile([P, S], F32, name="h%d" % t)
-            banks = [(s0, s1) for s0, s1 in zip(FIRST_TILE_CUTS, FIRST_TILE_CUTS[1:])] if t == 0 else OTHER_TILE_BANKS
-            if t == 1:
-                banks = [(0, 256), (256, BANK, LATE), (LATE, S)]
+            banks = [(0, 256), (256, BANK, LATE), (LATE, S)] if t < 2 else OTHER_TILE_BANKS
             for cuts in banks:
                 acc = psum_h.tile([P, BANK], F32)
                 for s0, s1 in zip(cuts, cuts[1:]):
@@ -151,9 +148,6 @@ def tile_picked_sagecat_max_p_kernel(
             gather(t == 0, c_planes[:, t * V : (t + 1) * V], t, cen_sb[:])
         nc.gpsimd.tensor_scalar(c_bf, c_planes.rearrange("p (t v) -> p v t", t=PACK), 1.0, 0.0, MULT, ADD)
 
-        for t in range(2):
-            for d in range(DEGREE):
-                gather(True, nb01[:, (t * DEGREE + d) * V : (t * DEGREE + d + 1) * V], t, pos_sb[d][:])
         nb23 = keep.tile([P, 2 * DEGREE * V], BF16, align_bytes=64)
         nb2 = nb23[:, : DEGREE * V]
         nb3 = nb23[:, DEGREE * V :]
@@ -161,11 +155,14 @@ def tile_picked_sagecat_max_p_kernel(
         def entries(d, v0, v1):
             return pos_sb[d][:, v0 // LIST_COLUMN : v1 // LIST_COLUMN]
 
+        for t in range(2):
+            for d in range(DEGREE):
+                gather(t == 0 or d < 2, nb01[:, (t * DEGREE + d) * V : (t * DEGREE + d + 1) * V], t, pos_sb[d][:])
         gather(True, nb2[:, :SHARED], 2, entries(0, 0, SHARED))
         for d in range(1, DEGREE):
             gather(False, nb2[:, d * V : (d + 1) * V], 2, pos_sb[d][:])
         for d in range(DEGREE):
-            gather(False, nb3[:, d * V : d * V + HALF], 3, entries(d, 0, HALF))
+            gather(True, nb3[:, d * V : d * V + HALF], 3, entries(d, 0, HALF))
         for d in range(2):
             gather(False, nb3[:, d * V + HALF : (d + 1) * V], 3, entries(d, HALF, V))
         gather(False, nb2[:, SHARED:V], 2, entries(0, SHARED, V))
@@ -180,8 +177,7 @@ def tile_picked_sagecat_max_p_kernel(
         cut = 2 * N + HALF
         nc.vector.quantize_mx(out=codes[:, :cut].bitcast(FP8X4), scales=scales[:, :cut], in_=second[:, : PACK * cut])
         pairs = nb23[:].rearrange("p (t w u v) -> p w t u v", t=2, w=2, u=2)
-        for t in range(2):
-            nc.vector.tensor_tensor(rounds[:, 2 + t, :, :HALF], pairs[:, 0, t, :, :HALF], pairs[:, 1, t, :, :HALF], MAX)
+        nc.vector.tensor_tensor(rounds[:, 2:, :, :HALF], pairs[:, 0, :, :, :HALF], pairs[:, 1, :, :, :HALF], MAX)
         nc.vector.quantize_mx(out=codes[:, cut:].bitcast(FP8X4), scales=scales[:, cut:], in_=second[:, PACK * cut :])
 
         accs = []

@@ -25,6 +25,8 @@ BANK = 512
 LIST_COLUMN = 16
 QUADRANT = 32
 SCALE_ROWS = 4
+EARLY = 512
+BLOCK_ROWS = 8
 RUN = 4
 LATE = 768
 SCALAR_SHARE = 12
@@ -50,28 +52,36 @@ def tile_picked_sagecat_max_p_kernel(
 
         table_scales = keep.tile([P, T], U8, align_bytes=64)
         nc.vector.memset(table_scales[:].bitcast(I32), 0)
+        x_sc = keep.tile([P, S], U8, align_bytes=64)
+        nc.vector.memset(x_sc[:].bitcast(I32), 0)
+        warm = keep.tile([P, 2], F32)
+        nc.gpsimd.memset(warm[:, :1], 0.0)
+        nc.scalar.activation(warm[:, 1:], warm[:, :1], COPY)
         offs_sb = load_list(offs, "offs_sb")
-        pos_sb = [load_list(pos1, "pos1_sb")]
-        for r in range(SCALE_ROWS):
-            nc.sync.dma_start(table_scales[r:P:QUADRANT, :].bitcast(I32), x_scales[0, r::SCALE_ROWS, :].bitcast(I32))
         table_words = keep.tile([P, T], U32, align_bytes=64, tag="words")
-        nc.sync.dma_start(table_words[:].bitcast(I32), x_words[0].rearrange("p c r -> p (c r)").bitcast(I32))
+        word_rows = x_words[0].rearrange("p c r -> p (c r)").bitcast(I32)
+        nc.sync.dma_start(table_words[:, :EARLY].bitcast(I32), word_rows[:, :EARLY])
+        nc.sync.dma_start(table_scales[0:P:BLOCK_ROWS, :].bitcast(I32), x_scales[0].bitcast(I32))
+        nc.sync.dma_start(table_words[:, EARLY:].bitcast(I32), word_rows[:, EARLY:])
+        cen_sb = load_list(cen, "cen_sb")
+        pos_sb = [load_list(pos1, "pos1_sb")]
         w1_raw = keep.tile([P, PACK, H], F32)
         nc.sync.dma_start(w1_raw[:], w1.rearrange("(p j) c -> p j c", j=PACK))
-        cen_sb = load_list(cen, "cen_sb")
         pos_sb.append(load_list(pos2, "pos2_sb"))
         pos_sb.append(load_list(pos3, "pos3_sb"))
         pos_sb.append(load_list(pos4, "pos4_sb"))
-        w23_raw = []
+
+        picked_sc = keep.tile([P, S], U8, align_bytes=64, tag="picked")
+        nc.vector.tensor_copy(picked_sc[:], table_scales[:].indirect(offs_sb[:]))
+        for r in range(SCALE_ROWS):
+            nc.scalar.dma_start(
+                x_sc[r:P:QUADRANT, :].bitcast(I32), picked_sc[BLOCK_ROWS * r : P : QUADRANT, :].bitcast(I32)
+            )
+        w23_raw = keep.tile([P, 2, PACK, N], F32, align_bytes=64, tag="picked")
         for a, w in enumerate((w3, w2)):
-            raw = keep.tile([P, PACK, N], F32, name="w23_raw%d" % a)
             rows = w.rearrange("(a t b) n -> b a t n", t=PACK, b=RUN)
             for b in range(RUN):
-                nc.sync.dma_start(raw[b:P:RUN], rows[b])
-            w23_raw.append(raw)
-
-        x_sc = keep.tile([P, S], U8, align_bytes=64)
-        nc.vector.tensor_copy(x_sc[:], table_scales[:].indirect(offs_sb[:]))
+                nc.sync.dma_start(w23_raw[b:P:RUN, a], rows[b])
         x_cd = keep.tile([P, LATE], U32, align_bytes=64)
         nc.vector.tensor_copy(x_cd[:], table_words[:].indirect(offs_sb[:, : LATE // LIST_COLUMN]))
 
@@ -138,7 +148,7 @@ def tile_picked_sagecat_max_p_kernel(
         w23_bf = second[:, : 2 * N * PACK].rearrange("p (a n j) -> p a n j", a=2, j=PACK)
         c_bf = second[:, 2 * N * PACK :].rearrange("p (v t) -> p v t", t=PACK)
         for a in range(2):
-            nc.gpsimd.tensor_scalar(w23_bf[:, a], w23_raw[a][:].rearrange("p j n -> p n j"), 1.0, 0.0, MULT, ADD)
+            nc.gpsimd.tensor_scalar(w23_bf[:, a], w23_raw[:, a].rearrange("p j n -> p n j"), 1.0, 0.0, MULT, ADD)
 
         work = keep.tile([P, 3 * PACK * V], BF16, align_bytes=64)
         c_planes = work[:, : PACK * V]

@@ -25,7 +25,6 @@ BANK = 512
 LIST_COLUMN = 16
 QUADRANT = 32
 SCALE_ROWS = 4
-EARLY = 512
 BLOCK_ROWS = 8
 RUN = 4
 LATE = 768
@@ -51,7 +50,10 @@ def tile_picked_sagecat_max_p_kernel(
             return tile
 
         table_scales = keep.tile([P, T], U8, align_bytes=64)
-        nc.vector.memset(table_scales[:].bitcast(I32), 0)
+        twice = x_scales[0].bitcast(I32).unsqueeze(1).to_broadcast([2 * BLOCK_ROWS, 2, T // 4])
+        nc.sync.dma_start(table_scales[:QUADRANT, :].bitcast(I32), twice)
+        nc.vector.memset(table_scales[QUADRANT : 2 * QUADRANT, :].bitcast(I32), 0)
+        nc.vector.memset(table_scales[2 * QUADRANT :, :].bitcast(I32), 0)
         x_sc = keep.tile([P, S], U8, align_bytes=64)
         nc.vector.memset(x_sc[:].bitcast(I32), 0)
         warm = keep.tile([P, 2], F32)
@@ -59,10 +61,7 @@ def tile_picked_sagecat_max_p_kernel(
         nc.scalar.activation(warm[:, 1:], warm[:, :1], COPY)
         offs_sb = load_list(offs, "offs_sb")
         table_words = keep.tile([P, T], U32, align_bytes=64, tag="words")
-        word_rows = x_words[0].rearrange("p c r -> p (c r)").bitcast(I32)
-        nc.sync.dma_start(table_words[:, :EARLY].bitcast(I32), word_rows[:, :EARLY])
-        nc.sync.dma_start(table_scales[0:P:BLOCK_ROWS, :].bitcast(I32), x_scales[0].bitcast(I32))
-        nc.sync.dma_start(table_words[:, EARLY:].bitcast(I32), word_rows[:, EARLY:])
+        nc.sync.dma_start(table_words[:].bitcast(I32), x_words[0].rearrange("p c r -> p (c r)").bitcast(I32))
         cen_sb = load_list(cen, "cen_sb")
         pos_sb = [load_list(pos1, "pos1_sb")]
         w1_raw = keep.tile([P, PACK, H], F32)
@@ -75,7 +74,7 @@ def tile_picked_sagecat_max_p_kernel(
         nc.vector.tensor_copy(picked_sc[:], table_scales[:].indirect(offs_sb[:]))
         for r in range(SCALE_ROWS):
             nc.scalar.dma_start(
-                x_sc[r:P:QUADRANT, :].bitcast(I32), picked_sc[BLOCK_ROWS * r : P : QUADRANT, :].bitcast(I32)
+                x_sc[r:P:QUADRANT, :].bitcast(I32), picked_sc[2 * r : QUADRANT : BLOCK_ROWS, :].bitcast(I32)
             )
         w23_raw = keep.tile([P, 2, PACK, N], F32, align_bytes=64, tag="picked")
         for a, w in enumerate((w3, w2)):

@@ -27,9 +27,9 @@ QUADRANT = 32
 SCALE_ROWS = 4
 BLOCK_ROWS = 8
 RUN = 4
-LATE = 768
+LATE = 896
 SCALAR_SHARE = 12
-OTHER_TILE_BANKS = [(0, BANK), (BANK, LATE, S)]
+OTHER_TILE_BANKS = [(0, BANK), (BANK, 768, LATE, S)]
 PIECES = ((0, 256), (256, 384), (384, V))
 SHARED = 256
 HALF = V // 2
@@ -118,7 +118,7 @@ def tile_picked_sagecat_max_p_kernel(
         h = []
         for t in range(PACK):
             ht = keep.tile([P, S], F32, name="h%d" % t)
-            banks = [(0, 256), (256, BANK, LATE), (LATE, S)] if t < 2 else OTHER_TILE_BANKS
+            banks = [(0, 256), (256, BANK, 768), (768, LATE, S)] if t < 2 else OTHER_TILE_BANKS
             for cuts in banks:
                 acc = psum_h.tile([P, BANK], F32)
                 for s0, s1 in zip(cuts, cuts[1:]):
@@ -131,7 +131,7 @@ def tile_picked_sagecat_max_p_kernel(
                         start=True,
                         stop=True,
                     )
-                if t == 1 and cuts[0] == 0:
+                if t == 0 and cuts[0] == 256:
                     nc.vector.tensor_scalar_max(ht[:, cuts[0] : cuts[-1]], acc[:, : cuts[-1] - cuts[0]], 0.0)
                 else:
                     nc.scalar.activation(ht[:, cuts[0] : cuts[-1]], acc[:, : cuts[-1] - cuts[0]], RELU)

@@ -41,24 +41,20 @@ def tile_picked_sagecat_max_p_kernel(
     nc = tc.nc
     with ExitStack() as ctx:
         keep = ctx.enter_context(tc.tile_pool(name="keep", bufs=1))
-        psum_h = ctx.enter_context(tc.psum_pool(name="psum_h", bufs=5))
-        psum_o = ctx.enter_context(tc.psum_pool(name="psum_o", bufs=3))
+        psum = ctx.enter_context(tc.psum_pool(name="psum", bufs=8))
 
         def load_list(src, name):
             tile = keep.tile(list(src.shape), U16, name=name)
             nc.sync.dma_start(tile[:], src)
             return tile
 
-        table_scales = keep.tile([P, T], U8, align_bytes=64)
+        table_scales = keep.tile([P, T], U8, align_bytes=64, tag="scales")
         twice = x_scales[0].bitcast(I32).unsqueeze(1).to_broadcast([2 * BLOCK_ROWS, 2, T // 4])
         nc.sync.dma_start(table_scales[:QUADRANT, :].bitcast(I32), twice)
         nc.vector.memset(table_scales[QUADRANT : 2 * QUADRANT, :].bitcast(I32), 0)
         nc.vector.memset(table_scales[2 * QUADRANT :, :].bitcast(I32), 0)
         x_sc = keep.tile([P, S], U8, align_bytes=64)
         nc.vector.memset(x_sc[:].bitcast(I32), 0)
-        warm = keep.tile([P, 2], F32)
-        nc.gpsimd.memset(warm[:, :1], 0.0)
-        nc.scalar.activation(warm[:, 1:], warm[:, :1], COPY)
         offs_sb = load_list(offs, "offs_sb")
         table_words = keep.tile([P, T], U32, align_bytes=64, tag="words")
         nc.sync.dma_start(table_words[:].bitcast(I32), x_words[0].rearrange("p c r -> p (c r)").bitcast(I32))
@@ -70,13 +66,13 @@ def tile_picked_sagecat_max_p_kernel(
         pos_sb.append(load_list(pos3, "pos3_sb"))
         pos_sb.append(load_list(pos4, "pos4_sb"))
 
-        picked_sc = keep.tile([P, S], U8, align_bytes=64, tag="picked")
+        picked_sc = keep.tile([P, S], U8, align_bytes=64)
         nc.vector.tensor_copy(picked_sc[:], table_scales[:].indirect(offs_sb[:]))
         for r in range(SCALE_ROWS):
-            nc.scalar.dma_start(
+            nc.sync.dma_start(
                 x_sc[r:P:QUADRANT, :].bitcast(I32), picked_sc[2 * r : QUADRANT : BLOCK_ROWS, :].bitcast(I32)
             )
-        w23_raw = keep.tile([P, 2, PACK, N], F32, align_bytes=64, tag="picked")
+        w23_raw = keep.tile([P, 2, PACK, N], F32, align_bytes=64, tag="scales")
         for a, w in enumerate((w3, w2)):
             rows = w.rearrange("(a t b) n -> b a t n", t=PACK, b=RUN)
             for b in range(RUN):
@@ -118,9 +114,9 @@ def tile_picked_sagecat_max_p_kernel(
         h = []
         for t in range(PACK):
             ht = keep.tile([P, S], F32, name="h%d" % t)
-            banks = [(0, 256), (256, BANK, 768), (768, LATE, S)] if t < 2 else OTHER_TILE_BANKS
+            banks = [(0, 256), (256, BANK, 768), (768, LATE, S)] if t == 0 else OTHER_TILE_BANKS
             for cuts in banks:
-                acc = psum_h.tile([P, BANK], F32)
+                acc = psum.tile([P, BANK], F32, tag="bank")
                 for s0, s1 in zip(cuts, cuts[1:]):
                     nc.tensor.matmul_mx(
                         out=acc[:, s0 - cuts[0] : s1 - cuts[0]],
@@ -191,7 +187,7 @@ def tile_picked_sagecat_max_p_kernel(
 
         accs = []
         for v0, v1 in PIECES:
-            acc_o = psum_o.tile([P, BANK], F32)
+            acc_o = psum.tile([P, BANK], F32, tag="bank")
             cols = slice(2 * N + v0, 2 * N + v1)
             nc.tensor.matmul_mx(
                 out=acc_o[:, : v1 - v0],

@@ -29,6 +29,10 @@ BLOCK_ROWS = 8
 RUN = 4
 LATE = 896
 SCALAR_SHARE = 12
+FIRST_TILE_BANKS = (
+    [(0, 256), (256, BANK), (BANK, 768), (768, LATE, S)],
+    [(0, 256), (256, BANK, 768), (768, LATE, S)],
+)
 OTHER_TILE_BANKS = [(0, BANK), (BANK, 768, LATE, S)]
 PIECES = ((0, 256), (256, 384), (384, V))
 SHARED = 256
@@ -111,10 +115,20 @@ def tile_picked_sagecat_max_p_kernel(
         quantise_w1(2, 3, w1_bf2[:])
         quantise_w1(3, 4, w1_bf3[:])
 
-        h = []
+        h = [keep.tile([P, S], F32, name="h%d" % t) for t in range(PACK)]
+
+        def gather(on_vector, dst, t, offsets):
+            if on_vector:
+                nc.vector.tensor_copy(dst, h[t][:].indirect(offsets))
+            else:
+                nc.scalar.activation(dst, h[t][:].indirect(offsets), COPY)
+
+        work = keep.tile([P, 3 * PACK * V], BF16, align_bytes=64)
+        c_planes = work[:, : PACK * V]
+        nb01 = work[:, PACK * V :]
         for t in range(PACK):
-            ht = keep.tile([P, S], F32, name="h%d" % t)
-            banks = [(0, 256), (256, BANK, 768), (768, LATE, S)] if t == 0 else OTHER_TILE_BANKS
+            ht = h[t]
+            banks = FIRST_TILE_BANKS[t] if t < 2 else OTHER_TILE_BANKS
             for cuts in banks:
                 acc = psum.tile([P, BANK], F32, tag="bank")
                 for s0, s1 in zip(cuts, cuts[1:]):
@@ -131,13 +145,8 @@ def tile_picked_sagecat_max_p_kernel(
                     nc.vector.tensor_scalar_max(ht[:, cuts[0] : cuts[-1]], acc[:, : cuts[-1] - cuts[0]], 0.0)
                 else:
                     nc.scalar.activation(ht[:, cuts[0] : cuts[-1]], acc[:, : cuts[-1] - cuts[0]], RELU)
-            h.append(ht)
-
-        def gather(on_vector, dst, t, offsets):
-            if on_vector:
-                nc.vector.tensor_copy(dst, h[t][:].indirect(offsets))
-            else:
-                nc.scalar.activation(dst, h[t][:].indirect(offsets), COPY)
+                if (t, cuts[0]) == (1, 0):
+                    gather(False, nb01[:, 3 * V : 4 * V], 0, pos_sb[3][:])
 
         second = keep.tile([P, 2 * N * PACK + V * PACK], BF16, align_bytes=64, tag="words")
         w23_bf = second[:, : 2 * N * PACK].rearrange("p (a n j) -> p a n j", a=2, j=PACK)
@@ -145,12 +154,9 @@ def tile_picked_sagecat_max_p_kernel(
         for a in range(2):
             nc.gpsimd.tensor_scalar(w23_bf[:, a], w23_raw[:, a].rearrange("p j n -> p n j"), 1.0, 0.0, MULT, ADD)
 
-        work = keep.tile([P, 3 * PACK * V], BF16, align_bytes=64)
-        c_planes = work[:, : PACK * V]
-        nb01 = work[:, PACK * V :]
         rounds = work[:, : 2 * PACK * V].rearrange("p (t u v) -> p t u v", t=PACK, u=2)
         for t in range(PACK):
-            gather(t == 0, c_planes[:, t * V : (t + 1) * V], t, cen_sb[:])
+            gather(t < 2, c_planes[:, t * V : (t + 1) * V], t, cen_sb[:])
         nc.gpsimd.tensor_scalar(c_bf, c_planes.rearrange("p (t v) -> p v t", t=PACK), 1.0, 0.0, MULT, ADD)
 
         nb23 = keep.tile([P, 2 * DEGREE * V], BF16, align_bytes=64)
@@ -161,7 +167,7 @@ def tile_picked_sagecat_max_p_kernel(
             return pos_sb[d][:, v0 // LIST_COLUMN : v1 // LIST_COLUMN]
 
         for t in range(2):
-            for d in range(DEGREE):
+            for d in range(DEGREE - 1 if t == 0 else DEGREE):
                 gather(t == 0 or d < 2, nb01[:, (t * DEGREE + d) * V : (t * DEGREE + d + 1) * V], t, pos_sb[d][:])
         gather(True, nb2[:, :SHARED], 2, entries(0, 0, SHARED))
         for d in range(1, DEGREE):

@@ -13,11 +13,14 @@ U16 = mybir.dt.uint16
 U8 = mybir.dt.uint8
 FP8X4 = mybir.dt.float8_e4m3fn_x4
 MAX = mybir.AluOpType.max
+MIN = mybir.AluOpType.min
 ADD = mybir.AluOpType.add
 MULT = mybir.AluOpType.mult
+SUBTRACT = mybir.AluOpType.subtract
 RELU = mybir.ActivationFunctionType.Relu
 COPY = mybir.ActivationFunctionType.Copy
 
+LARGEST = 3.4028234663852886e38
 P = 128
 PACK = 4
 DEGREE = 4
@@ -35,7 +38,8 @@ FIRST_TILE_BANKS = (
 )
 OTHER_TILE_BANKS = [(0, BANK), (BANK, 768, LATE, S)]
 PIECES = ((0, 256), (256, 384), (384, V))
-SHARED = 256
+SHARED = 288
+LENT = 256
 HALF = V // 2
 
 
@@ -123,9 +127,13 @@ def tile_picked_sagecat_max_p_kernel(
             else:
                 nc.scalar.activation(dst, h[t][:].indirect(offsets), COPY)
 
-        work = keep.tile([P, 3 * PACK * V], BF16, align_bytes=64)
-        c_planes = work[:, : PACK * V]
-        nb01 = work[:, PACK * V :]
+        work = keep.tile([P, 12 * V], BF16, align_bytes=64)
+        c_planes = work[:, 2 * V : 6 * V]
+        nb01 = work[:, 6 * V :].rearrange("p (w x v) -> p w x v", w=2, x=3)
+        second = keep.tile([P, 2 * N * PACK + V * PACK], BF16, align_bytes=64, tag="words")
+        w23_bf = second[:, : 2 * N * PACK].rearrange("p (a n j) -> p a n j", a=2, j=PACK)
+        c_bf = second[:, 2 * N * PACK :].rearrange("p (v t) -> p v t", t=PACK)
+        nb0 = second[:, 2 * N * PACK : 2 * N * PACK + 2 * V].rearrange("p (w v) -> p w v", w=2)
         for t in range(PACK):
             ht = h[t]
             banks = FIRST_TILE_BANKS[t] if t < 2 else OTHER_TILE_BANKS
@@ -146,15 +154,25 @@ def tile_picked_sagecat_max_p_kernel(
                 else:
                     nc.scalar.activation(ht[:, cuts[0] : cuts[-1]], acc[:, : cuts[-1] - cuts[0]], RELU)
                 if (t, cuts[0]) == (1, 0):
-                    gather(False, nb01[:, 3 * V : 4 * V], 0, pos_sb[3][:])
+                    gather(False, nb0[:, 1], 0, pos_sb[3][:])
 
-        second = keep.tile([P, 2 * N * PACK + V * PACK], BF16, align_bytes=64, tag="words")
-        w23_bf = second[:, : 2 * N * PACK].rearrange("p (a n j) -> p a n j", a=2, j=PACK)
-        c_bf = second[:, 2 * N * PACK :].rearrange("p (v t) -> p v t", t=PACK)
         for a in range(2):
             nc.gpsimd.tensor_scalar(w23_bf[:, a], w23_raw[:, a].rearrange("p j n -> p n j"), 1.0, 0.0, MULT, ADD)
 
         rounds = work[:, : 2 * PACK * V].rearrange("p (t u v) -> p t u v", t=PACK, u=2)
+        gather(True, nb0[:, 0], 0, pos_sb[0][:])
+        for w in range(2):
+            gather(True, nb01[:, w, 0], 0, pos_sb[1 + w][:])
+
+        def largest_on_gpsimd(dst, low, high, gap):
+            nc.gpsimd.tensor_tensor(gap, high, low, SUBTRACT)
+            nc.gpsimd.tensor_scalar(gap, gap, LARGEST, 0.0, MIN, MAX)
+            nc.gpsimd.tensor_tensor(dst, gap, low, ADD)
+
+        first_gap = keep.tile([P, V], F32, align_bytes=64, tag="scales")
+        largest_on_gpsimd(rounds[:, 0, 0], nb0[:, 0], nb0[:, 1], first_gap[:])
+        second_gap = second[:, 2 * N * PACK : 2 * N * PACK + 2 * LENT].bitcast(F32)
+        largest_on_gpsimd(rounds[:, 0, 1, :LENT], nb01[:, 0, 0, :LENT], nb01[:, 1, 0, :LENT], second_gap)
         for t in range(PACK):
             gather(t < 2, c_planes[:, t * V : (t + 1) * V], t, cen_sb[:])
         nc.gpsimd.tensor_scalar(c_bf, c_planes.rearrange("p (t v) -> p v t", t=PACK), 1.0, 0.0, MULT, ADD)
@@ -166,9 +184,8 @@ def tile_picked_sagecat_max_p_kernel(
         def entries(d, v0, v1):
             return pos_sb[d][:, v0 // LIST_COLUMN : v1 // LIST_COLUMN]
 
-        for t in range(2):
-            for d in range(DEGREE - 1 if t == 0 else DEGREE):
-                gather(t == 0 or d < 2, nb01[:, (t * DEGREE + d) * V : (t * DEGREE + d + 1) * V], t, pos_sb[d][:])
+        for d in range(DEGREE):
+            gather(d < 2, nb01[:, d // 2, 1 + d % 2], 1, pos_sb[d][:])
         gather(True, nb2[:, :SHARED], 2, entries(0, 0, SHARED))
         for d in range(1, DEGREE):
             gather(False, nb2[:, d * V : (d + 1) * V], 2, pos_sb[d][:])
@@ -179,8 +196,7 @@ def tile_picked_sagecat_max_p_kernel(
         gather(False, nb2[:, SHARED:V], 2, entries(0, SHARED, V))
         gather(False, nb3[:, 2 * V + HALF : 3 * V], 3, entries(2, HALF, V))
 
-        both = nb01.rearrange("p (t u x) -> p t u x", t=2, u=2)
-        nc.vector.tensor_tensor(c_planes.rearrange("p (t x) -> p t x", t=2), both[:, :, 0], both[:, :, 1], MAX)
+        nc.vector.tensor_tensor(work[:, V + LENT : 4 * V], work[:, 6 * V + LENT : 9 * V], work[:, 9 * V + LENT :], MAX)
         for v0, v1 in PIECES[1:]:
             gather(False, rounds[:, 3, 1, v0:v1], 3, entries(3, v0, v1))
         codes = keep.tile([P, 2 * N + V], U32, align_bytes=64)
@@ -188,7 +204,8 @@ def tile_picked_sagecat_max_p_kernel(
         cut = 2 * N + HALF
         nc.vector.quantize_mx(out=codes[:, :cut].bitcast(FP8X4), scales=scales[:, :cut], in_=second[:, : PACK * cut])
         pairs = nb23[:].rearrange("p (t w u v) -> p w t u v", t=2, w=2, u=2)
-        nc.vector.tensor_tensor(rounds[:, 2:, :, :HALF], pairs[:, 0, :, :, :HALF], pairs[:, 1, :, :, :HALF], MAX)
+        nc.vector.tensor_tensor(rounds[:, 3, :, :HALF], pairs[:, 0, 1, :, :HALF], pairs[:, 1, 1, :, :HALF], MAX)
+        nc.vector.tensor_tensor(rounds[:, 2, :, :HALF], pairs[:, 0, 0, :, :HALF], pairs[:, 1, 0, :, :HALF], MAX)
         nc.vector.quantize_mx(out=codes[:, cut:].bitcast(FP8X4), scales=scales[:, cut:], in_=second[:, PACK * cut :])
 
         accs = []

@@ -38,7 +38,7 @@ FIRST_TILE_BANKS = (
 )
 OTHER_TILE_BANKS = [(0, BANK), (BANK, 768, LATE, S)]
 PIECES = ((0, 256), (256, 384), (384, V))
-SHARED = 288
+SHARED = 352
 LENT = 256
 HALF = V // 2
 

@@ -49,6 +49,7 @@ def tile_picked_sagecat_max_p_kernel(
     nc = tc.nc
     with ExitStack() as ctx:
         keep = ctx.enter_context(tc.tile_pool(name="keep", bufs=1))
+        shared = ctx.enter_context(tc.tile_pool(name="shared", bufs=1))
         psum = ctx.enter_context(tc.psum_pool(name="psum", bufs=8))
 
         def load_list(src, name):
@@ -56,13 +57,11 @@ def tile_picked_sagecat_max_p_kernel(
             nc.sync.dma_start(tile[:], src)
             return tile
 
-        table_scales = keep.tile([P, T], U8, align_bytes=64, tag="scales")
+        table_scales = shared.tile([P, T], U8, align_bytes=64, offset=0)
         twice = x_scales[0].bitcast(I32).unsqueeze(1).to_broadcast([2 * BLOCK_ROWS, 2, T // 4])
         nc.sync.dma_start(table_scales[:QUADRANT, :].bitcast(I32), twice)
         nc.vector.memset(table_scales[QUADRANT : 2 * QUADRANT, :].bitcast(I32), 0)
         nc.vector.memset(table_scales[2 * QUADRANT :, :].bitcast(I32), 0)
-        x_sc = keep.tile([P, S], U8, align_bytes=64)
-        nc.vector.memset(x_sc[:].bitcast(I32), 0)
         offs_sb = load_list(offs, "offs_sb")
         table_words = keep.tile([P, T], U32, align_bytes=64, tag="words")
         nc.sync.dma_start(table_words[:].bitcast(I32), x_words[0].rearrange("p c r -> p (c r)").bitcast(I32))
@@ -76,11 +75,12 @@ def tile_picked_sagecat_max_p_kernel(
 
         picked_sc = keep.tile([P, S], U8, align_bytes=64)
         nc.vector.tensor_copy(picked_sc[:], table_scales[:].indirect(offs_sb[:]))
+        x_sc = shared.tile([P, S], U8, align_bytes=64, offset=0)
         for r in range(SCALE_ROWS):
             nc.sync.dma_start(
                 x_sc[r:P:QUADRANT, :].bitcast(I32), picked_sc[2 * r : QUADRANT : BLOCK_ROWS, :].bitcast(I32)
             )
-        w23_raw = keep.tile([P, 2, PACK, N], F32, align_bytes=64, tag="scales")
+        w23_raw = shared.tile([P, 2, PACK, N], F32, align_bytes=64, offset=S)
         for a, w in enumerate((w3, w2)):
             rows = w.rearrange("(a t b) n -> b a t n", t=PACK, b=RUN)
             for b in range(RUN):
@@ -169,7 +169,7 @@ def tile_picked_sagecat_max_p_kernel(
             nc.gpsimd.tensor_scalar(gap, gap, LARGEST, 0.0, MIN, MAX)
             nc.gpsimd.tensor_tensor(dst, gap, low, ADD)
 
-        first_gap = keep.tile([P, V], F32, align_bytes=64, tag="scales")
+        first_gap = shared.tile([P, V], F32, align_bytes=64, offset=S)
         largest_on_gpsimd(rounds[:, 0, 0], nb0[:, 0], nb0[:, 1], first_gap[:])
         second_gap = second[:, 2 * N * PACK : 2 * N * PACK + 2 * LENT].bitcast(F32)
         largest_on_gpsimd(rounds[:, 0, 1, :LENT], nb01[:, 0, 0, :LENT], nb01[:, 1, 0, :LENT], second_gap)

@@ -40,6 +40,7 @@ OTHER_TILE_BANKS = [(0, BANK), (BANK, 768, LATE, S)]
 PIECES = ((0, 256), (256, 384), (384, V))
 SHARED = 352
 LENT = 256
+APART = 32768
 HALF = V // 2
 
 
@@ -50,6 +51,7 @@ def tile_picked_sagecat_max_p_kernel(
     with ExitStack() as ctx:
         keep = ctx.enter_context(tc.tile_pool(name="keep", bufs=1))
         shared = ctx.enter_context(tc.tile_pool(name="shared", bufs=1))
+        spread = ctx.enter_context(tc.tile_pool(name="spread", bufs=1))
         psum = ctx.enter_context(tc.psum_pool(name="psum", bufs=8))
 
         def load_list(src, name):
@@ -119,7 +121,7 @@ def tile_picked_sagecat_max_p_kernel(
         quantise_w1(2, 3, w1_bf2[:])
         quantise_w1(3, 4, w1_bf3[:])
 
-        h = [keep.tile([P, S], F32, name="h%d" % t) for t in range(PACK)]
+        h = [spread.tile([P, S], F32, name="h%d" % t, offset=(t + 1) * APART) for t in range(PACK)]
 
         def gather(on_vector, dst, t, offsets):
             if on_vector:

from contextlib import ExitStack

import concourse.mybir as mybir

K, T, S, V, H, N = 512, 2048, 1024, 512, 512, 128
FLOPS = 2 * K * H * S + 2 * 2 * H * N * V

F32 = mybir.dt.float32
BF16 = mybir.dt.bfloat16
I32 = mybir.dt.int32
U32 = mybir.dt.uint32
U16 = mybir.dt.uint16
U8 = mybir.dt.uint8
FP8X4 = mybir.dt.float8_e4m3fn_x4
MAX = mybir.AluOpType.max
MIN = mybir.AluOpType.min
ADD = mybir.AluOpType.add
MULT = mybir.AluOpType.mult
SUBTRACT = mybir.AluOpType.subtract
RELU = mybir.ActivationFunctionType.Relu
COPY = mybir.ActivationFunctionType.Copy

LARGEST = 3.4028234663852886e38
P = 128
PACK = 4
DEGREE = 4
BANK = 512
LIST_COLUMN = 16
QUADRANT = 32
SCALE_ROWS = 4
BLOCK_ROWS = 8
RUN = 4
LATE = 896
SCALAR_SHARE = 12
FIRST_TILE_BANKS = (
    [(0, 256), (256, BANK), (BANK, 768), (768, LATE, S)],
    [(0, 256), (256, BANK, 768), (768, LATE, S)],
)
OTHER_TILE_BANKS = [(0, BANK), (BANK, 768, LATE, S)]
PIECES = ((0, 256), (256, 384), (384, V))
SHARED = 352
LENT = 256
APART = 32768
HALF = V // 2


def tile_picked_sagecat_max_p_kernel(
    tc, x_words, x_scales, w1, w2, w3, offs, cen, pos1, pos2, pos3, pos4, out
):
    nc = tc.nc
    with ExitStack() as ctx:
        keep = ctx.enter_context(tc.tile_pool(name="keep", bufs=1))
        shared = ctx.enter_context(tc.tile_pool(name="shared", bufs=1))
        spread = ctx.enter_context(tc.tile_pool(name="spread", bufs=1))
        psum = ctx.enter_context(tc.psum_pool(name="psum", bufs=8))

        def load_list(src, name):
            tile = keep.tile(list(src.shape), U16, name=name)
            nc.sync.dma_start(tile[:], src)
            return tile

        table_scales = shared.tile([P, T], U8, align_bytes=64, offset=0)
        twice = x_scales[0].bitcast(I32).unsqueeze(1).to_broadcast([2 * BLOCK_ROWS, 2, T // 4])
        nc.sync.dma_start(table_scales[:QUADRANT, :].bitcast(I32), twice)
        nc.vector.memset(table_scales[QUADRANT : 2 * QUADRANT, :].bitcast(I32), 0)
        nc.vector.memset(table_scales[2 * QUADRANT :, :].bitcast(I32), 0)
        offs_sb = load_list(offs, "offs_sb")
        table_words = keep.tile([P, T], U32, align_bytes=64, tag="words")
        nc.sync.dma_start(table_words[:].bitcast(I32), x_words[0].rearrange("p c r -> p (c r)").bitcast(I32))
        cen_sb = load_list(cen, "cen_sb")
        pos_sb = [load_list(pos1, "pos1_sb")]
        w1_raw = keep.tile([P, PACK, H], F32)
        nc.sync.dma_start(w1_raw[:], w1.rearrange("(p j) c -> p j c", j=PACK))
        pos_sb.append(load_list(pos2, "pos2_sb"))
        pos_sb.append(load_list(pos3, "pos3_sb"))
        pos_sb.append(load_list(pos4, "pos4_sb"))

        picked_sc = keep.tile([P, S], U8, align_bytes=64)
        nc.vector.tensor_copy(picked_sc[:], table_scales[:].indirect(offs_sb[:]))
        x_sc = shared.tile([P, S], U8, align_bytes=64, offset=0)
        for r in range(SCALE_ROWS):
            nc.sync.dma_start(
                x_sc[r:P:QUADRANT, :].bitcast(I32), picked_sc[2 * r : QUADRANT : BLOCK_ROWS, :].bitcast(I32)
            )
        w23_raw = shared.tile([P, 2, PACK, N], F32, align_bytes=64, offset=S)
        for a, w in enumerate((w3, w2)):
            rows = w.rearrange("(a t b) n -> b a t n", t=PACK, b=RUN)
            for b in range(RUN):
                nc.sync.dma_start(w23_raw[b:P:RUN, a], rows[b])
        x_cd = keep.tile([P, LATE], U32, align_bytes=64)
        nc.vector.tensor_copy(x_cd[:], table_words[:].indirect(offs_sb[:, : LATE // LIST_COLUMN]))

        dealt = w1_raw[:].rearrange("p j (a t b) -> p t a j b", t=PACK, b=RUN)

        def cast_view(tile):
            return tile[:].rearrange("p t (a b) j -> p t a j b", b=RUN)

        w1_cd = keep.tile([P, H], U32, align_bytes=64)
        w1_sc = keep.tile([P, H], U8, align_bytes=64)

        def quantise_w1(t0, t1, src):
            nc.vector.quantize_mx(
                out=w1_cd[:, t0 * P : t1 * P].bitcast(FP8X4),
                scales=w1_sc[:, t0 * P : t1 * P],
                in_=src.rearrange("p t m j -> p (t m j)"),
            )

        w1_bf0 = keep.tile([P, 1, P, PACK], BF16, align_bytes=64, tag="first")
        w1_bf1 = keep.tile([P, 1, P, PACK], BF16, align_bytes=64)
        w1_bf2 = keep.tile([P, 1, P, PACK], BF16, align_bytes=64)
        nc.scalar.copy(cast_view(w1_bf0)[:, 0, :SCALAR_SHARE], dealt[:, 0, :SCALAR_SHARE])
        nc.vector.tensor_copy(cast_view(w1_bf0)[:, 0, SCALAR_SHARE:], dealt[:, 0, SCALAR_SHARE:])
        quantise_w1(0, 1, w1_bf0[:])
        x_late = keep.tile([P, S - LATE], U32, align_bytes=64, tag="first")
        nc.vector.tensor_copy(x_late[:], table_words[:].indirect(offs_sb[:, LATE // LIST_COLUMN :]))
        nc.scalar.copy(cast_view(w1_bf1)[:, 0], dealt[:, 1])
        nc.scalar.copy(cast_view(w1_bf2)[:, 0], dealt[:, 2])
        quantise_w1(1, 2, w1_bf1[:])
        w1_bf3 = keep.tile([P, 1, P, PACK], BF16, align_bytes=64, tag="words")
        nc.vector.tensor_copy(cast_view(w1_bf3)[:, 0], dealt[:, 3])
        quantise_w1(2, 3, w1_bf2[:])
        quantise_w1(3, 4, w1_bf3[:])

        h = [spread.tile([P, S], F32, name="h%d" % t, offset=(t + 1) * APART) for t in range(PACK)]

        def gather(on_vector, dst, t, offsets):
            if on_vector:
                nc.vector.tensor_copy(dst, h[t][:].indirect(offsets))
            else:
                nc.scalar.activation(dst, h[t][:].indirect(offsets), COPY)

        work = keep.tile([P, 12 * V], BF16, align_bytes=64)
        c_planes = work[:, 2 * V : 6 * V]
        nb01 = work[:, 6 * V :].rearrange("p (w x v) -> p w x v", w=2, x=3)
        second = keep.tile([P, 2 * N * PACK + V * PACK], BF16, align_bytes=64, tag="words")
        w23_bf = second[:, : 2 * N * PACK].rearrange("p (a n j) -> p a n j", a=2, j=PACK)
        c_bf = second[:, 2 * N * PACK :].rearrange("p (v t) -> p v t", t=PACK)
        nb0 = second[:, 2 * N * PACK : 2 * N * PACK + 2 * V].rearrange("p (w v) -> p w v", w=2)
        for t in range(PACK):
            ht = h[t]
            banks = FIRST_TILE_BANKS[t] if t < 2 else OTHER_TILE_BANKS
            for cuts in banks:
                acc = psum.tile([P, BANK], F32, tag="bank")
                for s0, s1 in zip(cuts, cuts[1:]):
                    nc.tensor.matmul_mx(
                        out=acc[:, s0 - cuts[0] : s1 - cuts[0]],
                        lhsT=w1_cd[:, t * P : (t + 1) * P].bitcast(FP8X4),
                        lhsT_scale=w1_sc[:, t * P : (t + 1) * P],
                        rhs=(x_cd[:, s0:s1] if s1 <= LATE else x_late[:, s0 - LATE : s1 - LATE]).bitcast(FP8X4),
                        rhs_scale=x_sc[:, s0:s1],
                        start=True,
                        stop=True,
                    )
                if t == 0 and cuts[0] == 256:
                    nc.vector.tensor_scalar_max(ht[:, cuts[0] : cuts[-1]], acc[:, : cuts[-1] - cuts[0]], 0.0)
                else:
                    nc.scalar.activation(ht[:, cuts[0] : cuts[-1]], acc[:, : cuts[-1] - cuts[0]], RELU)
                if (t, cuts[0]) == (1, 0):
                    gather(False, nb0[:, 1], 0, pos_sb[3][:])

        for a in range(2):
            nc.gpsimd.tensor_scalar(w23_bf[:, a], w23_raw[:, a].rearrange("p j n -> p n j"), 1.0, 0.0, MULT, ADD)

        rounds = work[:, : 2 * PACK * V].rearrange("p (t u v) -> p t u v", t=PACK, u=2)
        gather(True, nb0[:, 0], 0, pos_sb[0][:])
        for w in range(2):
            gather(True, nb01[:, w, 0], 0, pos_sb[1 + w][:])

        def largest_on_gpsimd(dst, low, high, gap):
            nc.gpsimd.tensor_tensor(gap, high, low, SUBTRACT)
            nc.gpsimd.tensor_scalar(gap, gap, LARGEST, 0.0, MIN, MAX)
            nc.gpsimd.tensor_tensor(dst, gap, low, ADD)

        first_gap = shared.tile([P, V], F32, align_bytes=64, offset=S)
        largest_on_gpsimd(rounds[:, 0, 0], nb0[:, 0], nb0[:, 1], first_gap[:])
        second_gap = second[:, 2 * N * PACK : 2 * N * PACK + 2 * LENT].bitcast(F32)
        largest_on_gpsimd(rounds[:, 0, 1, :LENT], nb01[:, 0, 0, :LENT], nb01[:, 1, 0, :LENT], second_gap)
        for t in range(PACK):
            gather(t < 2, c_planes[:, t * V : (t + 1) * V], t, cen_sb[:])
        nc.gpsimd.tensor_scalar(c_bf, c_planes.rearrange("p (t v) -> p v t", t=PACK), 1.0, 0.0, MULT, ADD)

        nb23 = keep.tile([P, 2 * DEGREE * V], BF16, align_bytes=64)
        nb2 = nb23[:, : DEGREE * V]
        nb3 = nb23[:, DEGREE * V :]

        def entries(d, v0, v1):
            return pos_sb[d][:, v0 // LIST_COLUMN : v1 // LIST_COLUMN]

        for d in range(DEGREE):
            gather(d < 2, nb01[:, d // 2, 1 + d % 2], 1, pos_sb[d][:])
        gather(True, nb2[:, :SHARED], 2, entries(0, 0, SHARED))
        for d in range(1, DEGREE):
            gather(False, nb2[:, d * V : (d + 1) * V], 2, pos_sb[d][:])
        for d in range(DEGREE):
            gather(True, nb3[:, d * V : d * V + HALF], 3, entries(d, 0, HALF))
        for d in range(2):
            gather(False, nb3[:, d * V + HALF : (d + 1) * V], 3, entries(d, HALF, V))
        gather(False, nb2[:, SHARED:V], 2, entries(0, SHARED, V))
        gather(False, nb3[:, 2 * V + HALF : 3 * V], 3, entries(2, HALF, V))

        nc.vector.tensor_tensor(work[:, V + LENT : 4 * V], work[:, 6 * V + LENT : 9 * V], work[:, 9 * V + LENT :], MAX)
        for v0, v1 in PIECES[1:]:
            gather(False, rounds[:, 3, 1, v0:v1], 3, entries(3, v0, v1))
        codes = keep.tile([P, 2 * N + V], U32, align_bytes=64)
        scales = keep.tile([P, 2 * N + V], U8, align_bytes=64)
        cut = 2 * N + HALF
        nc.vector.quantize_mx(out=codes[:, :cut].bitcast(FP8X4), scales=scales[:, :cut], in_=second[:, : PACK * cut])
        pairs = nb23[:].rearrange("p (t w u v) -> p w t u v", t=2, w=2, u=2)
        nc.vector.tensor_tensor(rounds[:, 3, :, :HALF], pairs[:, 0, 1, :, :HALF], pairs[:, 1, 1, :, :HALF], MAX)
        nc.vector.tensor_tensor(rounds[:, 2, :, :HALF], pairs[:, 0, 0, :, :HALF], pairs[:, 1, 0, :, :HALF], MAX)
        nc.vector.quantize_mx(out=codes[:, cut:].bitcast(FP8X4), scales=scales[:, cut:], in_=second[:, PACK * cut :])

        accs = []
        for v0, v1 in PIECES:
            acc_o = psum.tile([P, BANK], F32, tag="bank")
            cols = slice(2 * N + v0, 2 * N + v1)
            nc.tensor.matmul_mx(
                out=acc_o[:, : v1 - v0],
                lhsT=codes[:, N : 2 * N].bitcast(FP8X4),
                lhsT_scale=scales[:, N : 2 * N],
                rhs=codes[:, cols].bitcast(FP8X4),
                rhs_scale=scales[:, cols],
                start=True,
                stop=False,
            )
            accs.append(acc_o)

        z_bfs = [keep.tile([P, (v1 - v0) * PACK], BF16, align_bytes=64, name="z_bf%d" % v0) for v0, v1 in PIECES]

        def last_round(e):
            v0, v1 = PIECES[e]
            nc.vector.tensor_tensor(
                z_bfs[e][:].rearrange("p (c i t) -> p c t i", i=RUN, t=PACK),
                rounds[:, :, 0, v0:v1].rearrange("p t (c i) -> p c t i", i=RUN),
                rounds[:, :, 1, v0:v1].rearrange("p t (c i) -> p c t i", i=RUN),
                MAX,
            )

        def finish(e, copy, queue):
            v0, v1 = PIECES[e]
            z_cd = keep.tile([P, v1 - v0], U32, align_bytes=64, name="z_cd%d" % e)
            z_sc = keep.tile([P, v1 - v0], U8, align_bytes=64, name="z_sc%d" % e)
            nc.vector.quantize_mx(out=z_cd[:].bitcast(FP8X4), scales=z_sc[:], in_=z_bfs[e][:])
            nc.tensor.matmul_mx(
                out=accs[e][:, : v1 - v0],
                lhsT=codes[:, :N].bitcast(FP8X4),
                lhsT_scale=scales[:, :N],
                rhs=z_cd[:].bitcast(FP8X4),
                rhs_scale=z_sc[:],
                start=False,
                stop=True,
            )
            res = keep.tile([P, v1 - v0], F32, name="res%d" % e)
            copy(res[:], accs[e][:, : v1 - v0])
            queue.dma_start(out[:, v0:v1], res[:])

        last_round(0)
        of_two = nb2[:, :HALF]
        nc.vector.tensor_tensor(of_two, nb3[:, HALF:V], nb3[:, V + HALF : 2 * V], MAX)
        nc.vector.tensor_tensor(rounds[:, 2, :, HALF:], pairs[:, 0, 0, :, HALF:], pairs[:, 1, 0, :, HALF:], MAX)
        nc.vector.tensor_tensor(rounds[:, 3, 0, HALF:], of_two, nb3[:, 2 * V + HALF : 3 * V], MAX)
        finish(0, nc.scalar.copy, nc.sync)
        last_round(1)
        last_round(2)
        finish(1, nc.scalar.copy, nc.scalar)
        finish(2, nc.vector.tensor_copy, nc.scalar)
